import numpy as np, ml_dtypes
CORES = [36,164,52,180,100,228,116,244]
N = 8
import mx_ref
BF = ml_dtypes.bfloat16
def gcols(t, e):
    v = np.concatenate([t.reshape(8, 16, -1, 4), np.zeros((8, 16, 1, 4), BF)], axis=2)
    return np.ascontiguousarray(np.stack([v[g][:, e[g]] for g in range(8)])).reshape(128, -1)
def tile(rs):
    return np.stack(rs, axis=2).reshape(128, -1).astype(BF)
def pick(q, e):
    c = np.concatenate([q[0].reshape(128, -1, 4), np.zeros((128, 1, 4), np.uint8)], axis=1); s = np.concatenate([q[1], np.ones((16, 1), np.uint8)], axis=1)
    return (np.ascontiguousarray(c[:, e].reshape(128, -1)), np.ascontiguousarray(s[:, e]))
def join(*qs):
    return (np.concatenate([q[0] for q in qs], axis=1), np.concatenate([q[1] for q in qs], axis=1))
def put(q, e, v):
    c, s = q[0].reshape(128, -1, 4).copy(), q[1].copy(); c[:, e] = v[0].reshape(128, -1, 4); s[:, e] = v[1]
    return (c.reshape(128, -1), s)
def pk(c, s):
    return (np.ascontiguousarray(c), mx_ref.live(s))
def emit(q):
    return q[0], q[1]
def packed(v, rng):
    q = [mx_ref.quantize(np.ascontiguousarray(v[r])) for r in range(N)]
    return np.stack([a for a, b in q]), np.stack([mx_ref.plane(b, rng) for a, b in q])
def values_of_codes():
    e, c = np.zeros((128, 128, 4), np.float32), np.zeros((128, 2, 4), np.uint8)
    e[np.arange(128), np.arange(128), 0] = 1
    c[:127, :, 0] = np.arange(256).reshape(2, 128).T[:127]
    return mx_ref.matmul(mx_ref.quantize(e.reshape(128, 512).astype(BF)), (c.reshape(128, 8), np.full((16, 2), 127, np.uint8))).T.reshape(-1).astype(np.float64)
CODE_VALUE, SCALE_VALUE = values_of_codes(), 2.0 ** (np.arange(256) - 127.0)
def decode(q):
    return (CODE_VALUE[q[0]].reshape(16, 8, -1, 4) * SCALE_VALUE[q[1]][:, None, :, None] + 0.0).reshape(128, -1).astype(np.float32)
def f(rng, *shape):
    return mx_ref.flush((rng.standard_normal(shape, dtype=np.float32) * np.exp2(rng.integers(-2, 3, shape[:-1] + (1,)))).astype(BF))
def wide(rng, *shape, cols=0):
    v = rng.standard_normal(shape, dtype=np.float32) * np.exp2(rng.integers(-12, 13, shape)).astype(np.float32)
    if cols: v *= np.repeat(np.exp2(rng.integers(-cols, cols + 1, shape[:-2] + (1, shape[-1] // 4))) * (rng.random(shape[:-2] + (1, shape[-1] // 4)) > 0.0625), 4, axis=-1).astype(np.float32)
    return mx_ref.flush(v.astype(BF))
C, M, R = 320, 160, 3
def meet(n):
    i = np.arange(n)
    q = np.stack([i] * 4 + [n - 1 - i] * 4)
    for h in range(1, 8):
        k = n // 2 if h < 4 else n // 2 - 1
        q[h, [h - 1, k]] = q[h, [k, h - 1]]
    q[4, [0, 1, 2, n - 1, n - 2, n - 3]] = q[4, [n - 1, n - 2, n - 3, 0, 1, 2]]
    return q
def big(v):
    v = v.astype(np.float32)
    v[np.abs(v) < np.float32(2.0 ** -16)] = 0
    return v.astype(BF)
def numbers_of(rng):
    return {"x": big(f(rng, N, 128, 4 * C)), "u": np.array(f(rng, N, 128, 512)), "v": np.array(f(rng, N, 128, 512))}
def layers(rng, still=[]):
    w = (rng.random((N, 128, 2048)) * 2.0 - 1.0) * 0.054 * np.exp2(-rng.integers(0, 2, (N, 128, 1)))
    w = big(w).reshape(N, 8, 16, 4, 8, 16, 4)
    for i in still:
        w[:, :, i] = 0
        w[:, :, :, :, :, i] = 0
    return w
def weights(rng, w):
    c, p = packed(np.ascontiguousarray(w).reshape(N, 128, 2048), rng)
    return {"wc": c, "ws": p}
def setup_inputs(rng):
    return {**numbers_of(rng), **weights(rng, layers(rng))}
def setup_inputs_ties(rng):
    d = numbers_of(rng)
    x = d["x"].reshape(N, 8, 16, C, 4)
    x[:, :, 0] = 0
    x[:, :, 0, :, 0] = rng.integers(1, 4, (N, 8, C)).astype(np.float32).astype(BF)
    u = d["u"].reshape(N, 128, 128, 4)
    one = u[:, :, :1].copy()
    one[:, :8] = 0
    u[:, :, ::16] = 0
    o = rng.permutation(N)
    for r in range(N):
        if o[r] == 2:
            u[r, :, ::16] = one[r]
            s = mx_ref.matmul(mx_ref.quantize(np.ascontiguousarray(u[r].reshape(128, 512))), mx_ref.quantize(np.ascontiguousarray(x[r].reshape(128, 4 * C))))[0]
            x[r, 0, 0] = 0
            x[r, 0, 0, np.argsort(-s, kind="stable")[C // 2], 0] = 2.0
            u[r, 0, 0, 0] = -2.0 ** 20
        else:
            for h in range(0, 128, 16): u[r, h, h, 0] = 0.0 if o[r] == 0 else -1.0 if o[r] == 1 else 1.0
    return {"x": x.reshape(N, 128, 4 * C), "u": u.reshape(N, 128, 512), "v": d["v"], **weights(rng, layers(rng, [0]))}
def setup_inputs_near(rng):
    d = numbers_of(rng)
    x = d["x"].astype(np.float32).reshape(N, 8, 16, C, 4)
    u = d["u"].reshape(N, 128, 128, 4)
    x[:, :, 0] = 0
    x[:, :, 8:] = 0
    u[:, :, ::16] = 0
    o = rng.permutation(N) % 4
    for r in range(N):
        k = 1.0 if o[r] == 0 else 2.0 ** -30
        if o[r] < 2:
            x[r, :, 0, :, 0] = rng.integers(0, 2, (8, C)) * 2.0 - 1.0
            x[r, :, 11, :, 0] = 2.0 ** -10
        if o[r] == 2:
            e = np.argsort(rng.random((8, C)), axis=1)
            x[r, :, 0, :, 0] = np.where(e < C // 16, 1.0, np.where(e < C // 8, -1.0, 0.0))
        if o[r] < 3:
            s = rng.integers(0, 16, (8, C))
            x[r, :, 8] = ((s[:, :, None] >> np.arange(4)) & 1) * np.exp2(np.arange(4) - 23.0)
        else:
            a = rng.integers(0, 4, (8, C))
            x[r, :, 10, :, 0] = np.array([1.0, 0.0, -1.0, 0.0])[a] * 2.0 ** -27
            x[r, :, 10, :, 1] = np.array([0.0, 1.125, 1.125, 0.0])[a] * 2.0 ** -27
        for h in range(0, 128, 16):
            if o[r] < 2:
                u[r, h, h, 0] = k
                u[r, h + 11, h, 0] = k
            if o[r] == 2: u[r, h, h, 0] = 1.0
            if o[r] < 3: u[r, h + 8, h] = k
            else:
                u[r, h + 10, h, 0] = 1.25 * k
                u[r, h + 10, h, 1] = 1.125 * k
    return {"x": x.reshape(N, 128, 4 * C).astype(BF), "u": u.reshape(N, 128, 512), "v": d["v"], **weights(rng, layers(rng, [0, 8, 9, 10, 11, 12, 13, 14, 15]))}
def setup_inputs_odd(rng):
    d = numbers_of(rng)
    a = (1.0 + (2 * rng.integers(0, 64, (N, 8, 2, C, 32)) + 1) * 2.0 ** -7) * np.exp2(-rng.integers(8, 15, (N, 8, 2, C, 32))) * (rng.integers(0, 2, (N, 8, 2, C, 32)) * 2.0 - 1.0)
    e = rng.integers(0, 32, (N, 8, 2, C, 1))
    np.put_along_axis(a, e, 1.96875 * (rng.integers(0, 2, (N, 8, 2, C, 1)) * 2.0 - 1.0), axis=4)
    a *= np.exp2(rng.integers(-1, 3, (N, 8, 2, C, 1)))
    d["x"] = np.ascontiguousarray(a.reshape(N, 8, 2, C, 8, 4).transpose(0, 1, 2, 4, 3, 5)).reshape(N, 128, 4 * C).astype(np.float32).astype(BF)
    return {**d, **weights(rng, layers(rng))}
def setup_inputs_ends(rng):
    d = numbers_of(rng)
    e = rng.permutation(N)
    o = e % 4
    x = (0.9 + 0.1 * rng.random((N, 8, 16, C, 4))) * 2.0 ** 30
    x[:, :, 8:] = 2.0 ** -27 * (rng.integers(0, 2, (N, 8, 8, C, 4)) * 2.0 - 1.0)
    u, v = d["u"].reshape(N, 128, 128, 4), d["v"]
    w = np.zeros((N, 8, 16, 4, 8, 16, 4), np.float32)
    for r in range(N):
        a = np.zeros((8, 16, 8, 4))
        if o[r] == 0: x[r] = -2.0 ** 30 * (0.9 + 0.1 * rng.random((8, 16, C, 4)))
        if o[r] == 1: x[r, :, :8] *= rng.integers(0, 2, (1, 1, C, 1)) * 2.0 - 1.0
        if o[r] == 2: x[r, :, :8] *= rng.integers(0, 2, (8, 8, C, 4)) * 2.0 - 1.0
        if o[r] == 3:
            q = meet(C)[rng.permutation(8)] if e[r] == 3 else np.stack([C - 1 - np.arange(C)] * 8)
            x[r, :, :8] *= rng.integers(0, 2, (8, 1, C, 1)) * 2.0 - 1.0
            x[r, :, 0] = 0
            x[r, :, 0, :, :3] = (((C - 1 - q)[:, :, None] >> np.array([0, 3, 6])) & 7) * 2.0 ** 27
            for g in range(0 if e[r] == 3 else 4, 8): a[g, 0, g, :3] = 2.0 ** 20 * np.array([1.0, 8.0, 64.0])
        if o[r] == 0: a = 2.0 ** 30 * (1.0 - 0.1 * rng.random((8, 16, 8, 4)))
        if o[r] == 1:
            a[:, :8] = 2.0 ** 30 * (1.0 - 0.1 * rng.random((8, 8, 8, 4)))
            a *= (rng.permutation(8) % 2 * 2.0 - 1.0)[None, None, :, None]
        if o[r] == 2: a[:, 8:] = 2.0 ** -30 * (rng.integers(0, 2, (8, 8, 8, 4)) * 2.0 - 1.0)
        u[r, :, ::16] = a.reshape(128, 8, 4).astype(np.float32).astype(BF)
        if o[r] == 0: w[r, :, :8, :, :, :8] = 0.0546875
        if o[r] in (1, 3): w[r, :, :8, :, :, :8] = 0.0546875 * (rng.integers(0, 2, (8, 8, 4, 8, 8, 4)) * 2.0 - 1.0)
        if o[r] == 0: v[r] = 2.0 ** 30
        if o[r] == 1: v[r] = (2.0 ** 30 * (rng.integers(0, 2, (128, 512)) * 2.0 - 1.0)).astype(np.float32).astype(BF)
        if o[r] == 2: v[r] = (2.0 ** -30 * (rng.integers(0, 2, (128, 512)) * 2.0 - 1.0)).astype(np.float32).astype(BF)
    return {"x": x.astype(np.float32).reshape(N, 128, 4 * C).astype(BF), "u": u.reshape(N, 128, 512), "v": v, **weights(rng, w.astype(BF))}
def setup_inputs_spread(rng):
    d = setup_inputs(rng)
    d["x"] = big(wide(rng, N, 128, 4 * C, cols=6))
    return d
def check_inputs(d):
    b = []
    for k, low in (("x", 2.0 ** -27), ("u", 2.0 ** -30), ("v", 2.0 ** -30)):
        a = np.abs(d[k].astype(np.float32))
        if not (np.isfinite(a).all() and ((a == 0) | (a >= low) & (a <= 2.0 ** 30)).all()): b.append("a value of " + k)
    none, least, most = [emit(mx_ref.quantize(np.full((128, 16), k, np.float32).astype(BF)))[1][0, 0] for k in (0.0, 2.0 ** -16, 2.0 ** -5)]
    for r in range(N):
        if ((d["wc"][r] == 0x7F) | (d["wc"][r] == 0xFF)).any(): b.append("wc: a code that is no number")
        s = mx_ref.live(d["ws"][r])
        if ((s != none) & ((s < least) | (s > most))).any(): b.append("ws: a scale out of range")
        if not (np.abs(decode(pk(d["wc"][r], d["ws"][r]))) < 2.0 ** -4).all(): b.append("wc, ws: a number of W that isn't below 2**-4 in size")
    return b
def reference(x, u, v, wc, ws):
    qu = [mx_ref.quantize(u[r]) for r in range(N)]
    lay = [pk(wc[r], ws[r]) for r in range(N)]
    now = [x[r] for r in range(N)]
    l, own = [None] * N, [None] * N
    for t in range(R):
        y, z = [], []
        for r in range(N):
            q = mx_ref.quantize(now[r])
            d = decode(q).astype(BF)
            s = mx_ref.matmul(qu[r], q)[::16] + np.float32(0.0)
            o = np.argsort(-s, axis=1, kind="stable")
            place = np.argsort(o, axis=1, kind="stable")
            m = np.sort(place, axis=0)
            l[r] = np.where(place <= m[3], o[:, m[4]], o[:, m[3]])
            c = np.argsort(m[0] - m[7], kind="stable")[:M]
            own[r] = l[r][:, c]
            z.append(mx_ref.quantize(gcols(d, own[r])))
            y.append(((now[r].astype(np.float32) + gcols(d, l[r]).astype(np.float32)) * np.float32(0.5)).astype(BF))
        for r in range(N):
            came = z[(r - 1 - t) % N]
            h = tile([mx_ref.matmul(pick(lay[r], np.arange(128 * b, 128 * b + 128)), came) * np.float32(0.03125) for b in range(4)])
            first = np.full((8, C), M)
            np.minimum.at(first, (np.arange(8)[:, None], own[r]), np.arange(M)[None])
            now[r] = gcols(np.concatenate([y[r], h], axis=1), np.where(first < M, C + first, np.arange(C)[None]))
    y, ol = np.zeros((N, 128, C), np.float32), np.zeros((N, 8, C), np.float32)
    oc, osc = np.zeros((N, 128, 4 * C), np.uint8), np.zeros((N, 16, C), np.uint8)
    for r in range(N):
        q = mx_ref.quantize(now[r])
        y[r] = mx_ref.matmul(mx_ref.quantize(v[r]), q)
        ol[r] = l[r]
        oc[r], osc[r] = emit(q)
    return {"y": y, "ol": ol, "oc": oc, "osc": osc}

@@ -1,0 +1,358 @@
+from concourse.mybir import dt, AluOpType, ActivationFunctionType
+
+A = AluOpType
+F = ActivationFunctionType
+C, M, R = 320, 160, 3
+MAGIC = 12582912.0
+BIG = 1.0e29
+NSCAN = 2
+SPEC = """x0 1280 b,x1 1280 b,x2 1280 b,x3 1280 b,uin 512 b,vin 512 b,qx 320 q,sx 320 s,qu 128 q,su 128 s,qu3 384 q,su3 384 s,
+qv 128 q,sv 128 s,wq 512 q,wp 512 s,ct 3584 b,qc 896 q,sc 896 s,ia 320 f,k16 320 f,c8 24 f,pi 4 i,pf 8 f,cj 4 f,ui 24 i,uoff 24 u,
+ident 128 b,gm 8 f,big 320 f,bigb 10x16 b,maskc 24 f,ioj 320 b,iom 320 b,iok 160 b,negj 320 f,r32 20x32 f,rt 20x32 f,w 640 f,
+tt 320 f,ds 20x16 f,cmp 20x336 b,junk 4x336 b,scan 4x168 f,q 20 f,qoff 20 u,qp 20 f,y0 20 f,m0 20 f,dig 80 b,mq 640 b,qm 160 q,
+sm 160 s,orow 320 b,qa 160 f,b1 2x80 f,ss 6x40 f,mn 2x40 f,mx 2x40 f,mn2 40 f,mx2 40 f,ma 20 f,mb 20 f,z0 20 f,woff 20 u,hi 20 f,
+lo 20 f,sp 24 f,spm 3x8 f,s4 3x4 f,s2 3x2 f,v3 4 f,y3 4 f,h3 4 f,l3 4 f,ok 4 f,kr 1280 b,qk 320 q,sk 320 s,key 320 f,cc 1280 b,
+qn 320 q,sn 320 s,rb 20x32 b,rbt 20x32 b,roff 20 u,lrow 320 b,lcrow 320 b,lb 10x32 b,lbt 10x32 b,lcb 10x16 b,lcw 10 f,lcoff 10 u,
+tp 1280 b,z 640 b,yb 20x32 b,ybt 20x32 b,lw 20 f,loff 20 u,dl 10x16 b,cd 10x176 b,dup 10 f,dof 10 f,doff 10 u,mw 2880 b,xb 20x32 b,
+xbt 20x32 b,mwf 20 f,moff 20 u,yt 1280 f,yh 1920 b,qz0 160 q,sz0 160 s,lq0 160 q,ls0 160 s,qz1 160 q,sz1 160 s,lq1 160 q,ls1 160 s,
+qz2 160 q,sz2 160 s,lq2 160 q,ls2 160 s"""
+KIND = {"b": "bfloat16", "f": "float32", "i": "int32", "u": "uint16", "q": "float8_e4m3fn_x4", "s": "uint8"}
+SCRATCH = {}
+for _e in SPEC.replace("\n", "").split(","):
+    _n, _s, _k = _e.split()
+    SCRATCH[_n] = ("sbuf", [128] + [int(v) for v in _s.split("x")], KIND[_k])
+for _n in ("psA", "psB", "psS", "psV"):
+    SCRATCH[_n] = ("psum", [128, 512], "float32")
+SCRATCH["psD"] = ("psum", [128, 2048], "float32")
+SEMAPHORES = ["eV", "eS", "eT", "eG"] + ["d%d" % i for i in range(16)] + ["sent%d" % t for t in range(R)] + ["came%d" % t for t in range(R)]
+
+
+def tracker(g, T):
+    queue = {"V": g.vector, "S": g.scalar, "T": g.tensor, "G": g, "Y": g.sync}
+    count, acc, known, hist, ndma = {}, {}, {q: {} for q in queue}, {}, [0]
+
+    def token(x):
+        return (x, 0, 1 << 30) if isinstance(x, str) else x
+
+    def learn(q, sem, val):
+        k = known[q]
+        if k.get(sem, 0) < val:
+            k[sem] = val
+        for s, v in hist.get((sem, val), {}).items():
+            if k.get(s, 0) < v:
+                k[s] = v
+
+    def waits(q, who, reads, writes):
+        req = {}
+        for toks, wr in ((reads, False), (writes, True)):
+            for name, lo, hi in map(token, toks):
+                for owner, sem, val, alo, ahi, aw in acc.get(name, ()):
+                    if alo >= hi or lo >= ahi:
+                        continue
+                    if not (aw or wr) and not (name.startswith("ps") and owner != who):
+                        continue
+                    if wr and not aw and owner == who:
+                        continue
+                    if who == "T" and owner == "T":
+                        continue
+                    req[sem] = max(req.get(sem, 0), val)
+        for sem, val in sorted(req.items(), key=lambda e: e[0]):
+            if known[q].get(sem, 0) < val:
+                queue[q].wait_ge(T.sem[sem], val)
+                learn(q, sem, val)
+
+    def note(q, who, sem, val, reads, writes):
+        hist[(sem, val)] = dict(known[q])
+        for toks, wr in ((reads, False), (writes, True)):
+            for name, lo, hi in map(token, toks):
+                acc.setdefault(name, []).append((who, sem, val, lo, hi, wr))
+
+    def op(q, fn, reads, writes):
+        waits(q, q, reads, writes)
+        sem = "e" + q
+        count[sem] = count.get(sem, 0) + 1
+        fn(queue[q]).then_inc(T.sem[sem], 1)
+        note(q, q, sem, count[sem], reads, writes)
+
+    def dma(q, out, in_, reads, writes):
+        sem = "d%d" % ndma[0]
+        ndma[0] += 1
+        waits(q, sem, reads, writes)
+        queue[q].dma_start(out, in_).then_inc(T.sem[sem], 16)
+        count[sem] = 16
+        note(q, sem, sem, 16, reads, writes)
+
+    def finish():
+        for sem in sorted(count):
+            g.wait_ge(T.sem[sem], count[sem])
+    return op, dma, waits, note, count, finish
+
+
+def rank_program(g, core, T, topo):
+    rank = T.rank_of(core)
+    if rank is None:
+        return
+    N = len(T.cores)
+    op, dma, waits, note, count, finish = tracker(g, T)
+
+    def copy(q, out, in_, rd, wr, scale=None):
+        if q == "S":
+            if scale is None:
+                op(q, lambda e: e.activation(out, in_, F.Copy), rd, wr)
+            else:
+                op(q, lambda e: e.activation(out, in_, F.Copy, scale=scale), rd, wr)
+        elif scale is None:
+            op(q, lambda e: e.tensor_copy(out, in_), rd, wr)
+        else:
+            op(q, lambda e: e.tensor_scalar(out, in_, scale, None, A.mult), rd, wr)
+
+    def ts(out, in_, s1, o1, rd, wr, s2=None, o2=None):
+        if o2 is None:
+            op("V", lambda e: e.tensor_scalar(out, in_, s1, None, o1), rd, wr)
+        else:
+            op("V", lambda e: e.tensor_scalar(out, in_, s1, s2, o1, o2), rd, wr)
+
+    def tt(out, a, b, o, rd, wr):
+        op("V", lambda e: e.tensor_tensor(out, a, b, o), rd, wr)
+
+    def quant(qn, sn, tn, n, q0=0):
+        op("V", lambda e: e.quantize_mx(T[qn][:, q0:q0 + n], T[sn][:, q0:q0 + n], T[tn][:, 4 * q0:4 * (q0 + n)]), [tn], [qn, sn])
+
+    def mm(out, otok, st, s0, mv, n):
+        lq, lp, rq, rp = T[st[0]], T[st[1]], T[mv[0]], T[mv[1]]
+        op("T", lambda e: e.matmul_mx(out, lq[:, s0:s0 + 128], lp[:, s0:s0 + 128], rq[:, 0:n], rp[:, 0:n], True, True),
+           [st[0], st[1], mv[0], mv[1]], [otok])
+
+    dma("Y", T.x0[:], T.x[:], [], ["x0"])
+    dma("S", T.uin[:], T.u[:], [], ["uin"])
+    dma("Y", T.wq[:].bitcast(dt.uint8), T.wc[:], [], ["wq"])
+    dma("S", T.wp[:], T.ws[:], [], ["wp"])
+    dma("Y", T.vin[:], T.v[:], [], ["vin"])
+
+    def iota(name, view, pat, base, cm, f=True):
+        if f:
+            op("G", lambda e: e.iota(view, pat, base, cm, allow_small_or_imprecise_dtypes=True), [], [name])
+        else:
+            op("G", lambda e: e.iota(view, pat, base, cm), [], [name])
+    iota("ui", T.ui[:, 0:8], [[16, 8]], 0, 0, False)
+    iota("ui", T.ui[:, 8:16], [[32, 4], [0, 2]], 0, 0, False)
+    iota("ui", T.ui[:, 16:24], [[32, 4], [0, 2]], 16, 0, False)
+    iota("pi", T.pi[:, 0:1], [[0, 1]], 0, 1, False)
+    iota("ia", T.ia[:], [[1, 320]], 0, 0)
+    iota("k16", T.k16[:], [[0, 20], [1, 16]], 0, 0)
+    iota("c8", T.c8[:], [[0, 3], [1, 8]], 0, 0)
+    iota("cj", T.cj[:, 0:3], [[-128, 3]], 0, -1)
+
+    def fill(view, name, v):
+        op("V", lambda e: e.memset(view, v), [], [name])
+    fill(T.ct[:], "ct", 0.0)
+    fill(T.ct[:, 2560:3072:4], "ct", 8192.0)
+    fill(T.ct[:, 2561:3072:4], "ct", 512.0)
+    fill(T.ct[:, 3072:3584], "ct", 1.0)
+    copy("V", T.uoff[:], T.ui[:], ["ui"], ["uoff"])
+    ts(T.pi[:, 1:2], T.pi[:, 0:1], 15, A.bitwise_and, [("pi", 0, 1)], [("pi", 1, 2)])
+    ts(T.pi[:, 2:3], T.pi[:, 0:1], 4, A.logical_shift_right, [("pi", 0, 1)], [("pi", 2, 3)])
+    ts(T.pi[:, 3:4], T.pi[:, 2:3], 1, A.bitwise_and, [("pi", 2, 3)], [("pi", 3, 4)])
+    copy("V", T.pf[:, 0:3], T.pi[:, 0:3], ["pi"], [("pf", 0, 3)])
+    copy("V", T.pf[:, 4:5], T.pi[:, 3:4], ["pi"], [("pf", 4, 5)])
+    ts(T.pf[:, 3:4], T.pf[:, 4:5], 0.0, A.is_equal, [("pf", 4, 5)], [("pf", 3, 4)])
+    pcol, kcol, gcol, even, odd = (T.pf[:, i:i + 1] for i in range(5))
+    quant("qu", "su", "uin", 128)
+    quant("qx", "sx", "x0", C)
+    for i in range(3):
+        op("V", lambda e: e.tensor_copy(T.qu3[:, 128 * i:128 * i + 128].bitcast(dt.uint32), T.qu[:, 0:128].bitcast(dt.uint32).indirect(T.uoff[:, 8 * i:8 * i + 8])), ["qu", "uoff"], [("qu3", 128 * i, 128 * i + 128)])
+        op("V", lambda e: e.tensor_copy(T.su3[:, 128 * i:128 * i + 128], T.su[:, 0:128].indirect(T.uoff[:, 8 * i:8 * i + 8])), ["su", "uoff"], [("su3", 128 * i, 128 * i + 128)])
+    ts(T.ident[:], T.ia[:, 0:128], pcol, A.is_equal, ["ia", "pf"], ["ident"])
+    for b in range(4):
+        copy("V" if b % 2 else "S", T.ct[:, 512 * b + b:512 * b + 512:4], T.ident[:], ["ident"], [("ct", 512 * b, 512 * b + 512)])
+    ts(T.big[:], T.k16[:], kcol, A.is_ge, ["k16", "pf"], ["big"], 2 * BIG, A.mult)
+    ts(T.big[:], T.big[:], -BIG, A.add, ["big"], ["big"])
+
+    def late_constants():
+        ts(T.ct[:, 2048:2560:4], T.k16[:, 0:128], kcol, A.is_equal, ["k16", "pf"], [("ct", 2048, 2560)], 16.0, A.mult)
+        ts(T.ct[:, 2049:2560:4], T.k16[:, 0:128], kcol, A.is_equal, ["k16", "pf"], [("ct", 2048, 2560)])
+        quant("qc", "sc", "ct", 512)
+        quant("qc", "sc", "ct", 384, 512)
+        ts(T.bigb[:], T.k16[:, 0:160], kcol, A.is_ge, ["k16", "pf"], ["bigb"], 2000.0, A.mult)
+        ts(T.bigb[:], T.bigb[:], -1000.0, A.add, ["bigb"], ["bigb"])
+        ts(T.gm[:], T.ia[:, 0:8], gcol, A.is_equal, ["ia", "pf"], ["gm"])
+        ts(T.maskc[:], T.c8[:], gcol, A.is_equal, ["c8", "pf"], ["maskc"])
+        ts(T.ioj[:], T.ia[:], -160.0, A.add, ["ia"], ["ioj"])
+        ts(T.iom[:], T.ia[:], -240.0, A.add, ["ia"], ["iom"])
+        ts(T.iok[:], T.ia[:, 0:160], 80.0, A.add, ["ia"], ["iok"])
+        ts(T.negj[:], T.ia[:], -1.0, A.mult, ["ia"], ["negj"])
+        fill(T.dig[:], "dig", 0.0)
+        fill(T.kr[:], "kr", 0.0)
+        fill(T.cc[:], "cc", 0.0)
+        fill(T.sp[:], "sp", 0.0)
+        quant("qv", "sv", "vin", 128)
+
+    QC, QU, QX = ("qc", "sc"), ("qu3", "su3"), ("qx", "sx")
+
+    def wrapped(row, rname, n, buf, bt):
+        copy("V", T[buf][:, 0:n, 0:16], row, [rname, "pf"], [(buf, 0, 1)], even)
+        copy("V", T[buf][:, 0:n, 16:32], row, [rname, "pf"], [(buf, 1, 2)], odd)
+        op("V", lambda e: e.transpose(T[bt][:], T[buf][:]), [buf], [bt])
+
+    for t in range(R):
+        xc, xn = "x%d" % t, "x%d" % (t + 1)
+        X = T[xc]
+        if t:
+            quant("qx", "sx", xc, C)
+        mm(T.psB[:, 0:C], "psB", QU, 256, QX, C)
+        mm(T.psA[:, 0:C], "psA", QU, 128, QX, C)
+        mm(T.psS[:, 0:C], "psS", QU, 0, QX, C)
+        mm(T.psV[:, 0:C], "psV", QU, 0, QX, C)
+        copy("V", T.r32[:, :, 16:32], T.psB[:, 0:C], ["psB"], [("r32", 1, 2)])
+        copy("S", T.r32[:, :, 0:16], T.psA[:, 0:C], ["psA"], [("r32", 0, 1)])
+        op("V", lambda e: e.transpose(T.rt[:], T.r32[:]), ["r32"], ["rt"])
+        op("S", lambda e: e.activation(T.tt[:], T.psS[:, 0:C], F.Abs, bias=2.0 ** -120, scale=1.25 * 2.0 ** -24), ["psS"], ["tt"])
+        copy("S", T.w[:, 0:C], T.psS[:, 0:C], ["psS"], [("w", 0, C)])
+        tt(T.ds[:], T.psV[:, 0:C], T.big[:], A.max, ["psV", "big"], ["ds"])
+        tt(T.cmp[:, :, 0:16], T.rt[:, :, 0:16], T.ds[:], A.is_equal, ["rt", "ds"], ["cmp"])
+        tt(T.w[:, C:2 * C], T.psV[:, 0:C], T.tt[:], A.add, ["psV", "tt"], [("w", C, 2 * C)])
+        ns = 0
+        for c in range(20):
+            ct = ("cmp", 336 * c, 336 * c + 336)
+            ts(T.cmp[:, c, 16:336], T.w[:, 16 * c:16 * c + C], T.rt[:, c, 0:1], A.is_gt, ["w", "rt"], [ct])
+            if c >= 20 - NSCAN:
+                op("V", lambda e: e.tensor_tensor_scan(T.scan[:, ns, :], T.cmp[:, c, 0:168], T.cmp[:, c, 168:336], 0.0, A.add, A.add), [ct], [("scan", ns, ns + 1)])
+                ns += 1
+            else:
+                op("S", lambda e: e.activation(T.junk[:, c % 4, :], T.cmp[:, c, :], F.Copy, accum_out=T.q[:, c:c + 1]), [ct], [("junk", c % 4, c % 4 + 1), ("q", c, c + 1)])
+        if t == 0:
+            late_constants()
+        if ns:
+            copy("V", T.q[:, 20 - ns:20], T.scan[:, 0:ns, 167], ["scan"], [("q", 20 - ns, 20)])
+        for b in range(4):
+            mm(T.psD[:, 512 * b:512 * b + C], ("psD", 512 * b, 512 * b + 512), QC, 128 * b, QX, C)
+        ts(T.y0[:], T.q[:], 0.0625, A.mult, ["q"], ["y0"], MAGIC, A.add)
+        ts(T.dig[:, 0:80:4], T.y0[:], -(MAGIC + 10), A.add, ["y0"], [("dig", 0, 1)])
+        ts(T.m0[:], T.y0[:], -MAGIC, A.add, ["y0"], ["m0"], -16.0, A.mult)
+        tt(T.dig[:, 1:80:4], T.q[:], T.m0[:], A.add, ["q", "m0"], [("dig", 1, 2)])
+        for h in range(8):
+            copy("S" if h % 3 == 1 else "V", T.mq[:, 80 * h:80 * h + 80], T.dig[:], ["dig", "gm"], [("mq", h, h + 1)], T.gm[:, h:h + 1])
+        quant("qm", "sm", "mq", M)
+        mm(T.psA[:, 0:M], "psA", QC, 512, ("qm", "sm"), M)
+        copy("V", T.qoff[:], T.q[:], ["q"], ["qoff"])
+        ts(T.qp[:], T.q[:], -160.0, A.add, ["q"], ["qp"])
+        op("V", lambda e: e.tensor_copy(T.orow[:, 0:C].indirect(T.qoff[:, 0:20]), T.ioj[:]), ["qoff", "ioj"], ["orow"])
+        for b in range(4):
+            copy("S", T.tp[:, C * b:C * b + C], T.psD[:, 512 * b:512 * b + C], [("psD", 512 * b, 512 * b + 512)], [("tp", C * b, C * b + C)])
+        copy("V", T.qa[:], T.psA[:, 0:M], ["psA"], ["qa"])
+        tt(T.b1[:, 0, :], T.qa[:, 0:80], T.qa[:, 80:160], A.min, ["qa"], [("b1", 0, 1)])
+        tt(T.b1[:, 1, :], T.qa[:, 0:80], T.qa[:, 80:160], A.max, ["qa"], [("b1", 1, 2)])
+        tt(T.ss[:, 0:4:3, :], T.b1[:, :, 0:40], T.b1[:, :, 40:80], A.max, ["b1"], [("ss", 0, 1), ("ss", 3, 4)])
+        tt(T.ss[:, 1:6:4, :], T.b1[:, :, 0:40], T.b1[:, :, 40:80], A.min, ["b1"], [("ss", 1, 2), ("ss", 5, 6)])
+        s = lambda i: ("ss", i, i + 1)
+        tt(T.hi[:], T.ss[:, 3, 0:20], T.ss[:, 3, 20:40], A.max, [s(3)], ["hi"])
+        tt(T.lo[:], T.ss[:, 1, 0:20], T.ss[:, 1, 20:40], A.min, [s(1)], ["lo"])
+        tt(T.ss[:, 2, :], T.ss[:, 0, :], T.ss[:, 5, :], A.min, [s(0), s(5)], [s(2)])
+        tt(T.sp[:, 0:20], T.hi[:], T.lo[:], A.subtract, ["hi", "lo"], ["sp"])
+        tt(T.ss[:, 4, :], T.ss[:, 0, :], T.ss[:, 5, :], A.max, [s(0), s(5)], [s(4)])
+        tt(T.spm[:], T.sp[:], T.maskc[:], A.mult, ["sp", "maskc"], ["spm"])
+        tt(T.mn[:, 0, :], T.ss[:, 1:3, 0:20], T.ss[:, 3:5, 20:40], A.min, ["ss"], [("mn", 0, 1)])
+        tt(T.s4[:], T.spm[:, :, 0:4], T.spm[:, :, 4:8], A.add, ["spm"], ["s4"])
+        tt(T.mn[:, 1, :], T.ss[:, 3:5, 0:20], T.ss[:, 1:3, 20:40], A.min, ["ss"], [("mn", 1, 2)])
+        tt(T.s2[:], T.s4[:, :, 0:2], T.s4[:, :, 2:4], A.add, ["s4"], ["s2"])
+        tt(T.mx[:, 0, :], T.ss[:, 1:3, 0:20], T.ss[:, 3:5, 20:40], A.max, ["ss"], [("mx", 0, 1)])
+        tt(T.v3[:, 0:3], T.s2[:, :, 0], T.s2[:, :, 1], A.add, ["s2"], ["v3"])
+        tt(T.mx[:, 1, :], T.ss[:, 3:5, 0:20], T.ss[:, 1:3, 20:40], A.max, ["ss"], [("mx", 1, 2)])
+        ts(T.y3[:, 0:3], T.v3[:, 0:3], 0.0625, A.mult, ["v3"], ["y3"], MAGIC, A.add)
+        tt(T.mn2[:], T.mn[:, 0, :], T.mn[:, 1, :], A.max, ["mn"], ["mn2"])
+        ts(T.h3[:, 0:3], T.y3[:, 0:3], -(MAGIC + 10), A.add, ["y3"], ["h3"])
+        ts(T.l3[:, 0:3], T.y3[:, 0:3], -MAGIC, A.add, ["y3"], ["l3"], -16.0, A.mult)
+        tt(T.mx2[:], T.mx[:, 0, :], T.mx[:, 1, :], A.min, ["mx"], ["mx2"])
+        tt(T.l3[:, 0:3], T.l3[:, 0:3], T.v3[:, 0:3], A.add, ["l3", "v3"], ["l3"])
+        for e3 in range(3):
+            n = min(128, C - 128 * e3)
+            a, z = 512 * e3, 512 * e3 + 4 * n
+            copy("V", T.kr[:, a:z:4], T.ident[:, 0:n], ["ident", "h3"], [("kr", 2 * e3, 2 * e3 + 1)], T.h3[:, e3:e3 + 1])
+            copy("S", T.kr[:, a + 1:z:4], T.ident[:, 0:n], ["ident", "l3"], [("kr", 2 * e3 + 1, 2 * e3 + 2)], T.l3[:, e3:e3 + 1])
+        quant("qk", "sk", "kr", C)
+        mm(T.psB[:, 0:C], "psB", QC, 640, ("qk", "sk"), C)
+        ts(T.ok[:, 0:3], T.v3[:, 0:3], -160.0, A.add, ["v3"], ["ok"], 512.0, A.mult)
+        tt(T.ma[:], T.mn2[:, 0:20], T.mn2[:, 20:40], A.max, ["mn2"], ["ma"])
+        tt(T.mb[:], T.mx2[:, 0:20], T.mx2[:, 20:40], A.min, ["mx2"], ["mb"])
+        tt(T.ok[:, 0:3], T.ok[:, 0:3], T.cj[:, 0:3], A.add, ["ok", "cj"], ["ok"])
+        tt(T.z0[:], T.ma[:], T.mb[:], A.add, ["ma", "mb"], ["z0"])
+        tt(T.z0[:], T.z0[:], T.qp[:], A.subtract, ["z0", "qp"], ["z0"])
+        tt(T.key[:], T.psB[:, 0:C], T.negj[:], A.add, ["psB", "negj"], ["key"])
+        tt(T.z0[:], T.z0[:], T.mb[:], A.min, ["z0", "mb"], ["z0"])
+        for e3 in range(3):
+            ts(T.cc[:, e3:1280:4], T.key[:], T.ok[:, e3:e3 + 1], A.is_lt, ["key", "ok"], [("cc", e3, e3 + 1)])
+        quant("qn", "sn", "cc", C)
+        mm(T.psS[:, 0:C], "psS", QC, 768, ("qn", "sn"), C)
+        tt(T.z0[:], T.z0[:], T.ma[:], A.max, ["z0", "ma"], ["z0"])
+        ts(T.woff[:], T.z0[:], 160.0, A.add, ["z0"], ["woff"])
+        op("V", lambda e: e.tensor_copy(T.lrow[:], T.orow[:, 0:C].indirect(T.woff[:, 0:20])), ["woff", "orow"], ["lrow"])
+        ts(T.rb[:, :, 0:16], T.psS[:, 0:C], -160.0, A.add, ["psS"], [("rb", 0, 1)])
+        copy("V", T.rb[:, :, 16:32], T.rb[:, :, 0:16], [("rb", 0, 1)], [("rb", 1, 2)])
+        op("V", lambda e: e.transpose(T.rbt[:], T.rb[:]), ["rb"], ["rbt"])
+        ts(T.roff[:], T.rbt[:, :, 0], 160.0, A.add, ["rbt"], ["roff"])
+        op("V", lambda e: e.tensor_copy(T.lcrow[:, 0:C].indirect(T.roff[:, 0:20]), T.lrow[:]), ["roff", "lrow"], ["lcrow"])
+        wrapped(T.lcrow[:, 0:M], "lcrow", 10, "lb", "lbt")
+        tt(T.lcw[:], T.lbt[:, :, 0], T.lbt[:, :, 16], A.add, ["lbt"], ["lcw"])
+        ts(T.lcoff[:], T.lcw[:], 160.0, A.add, ["lcw"], ["lcoff"])
+        for b in range(4):
+            copy("V" if b % 2 else "S", T.z[:, b:640:4], T.tp[:, C * b:C * b + C].indirect(T.lcoff[:, 0:10]), ["lcoff", ("tp", C * b, C * b + C)], [("z", b, b + 1)])
+        qz, sz, lq, lp = "qz%d" % t, "sz%d" % t, "lq%d" % t, "ls%d" % t
+        quant(qz, sz, "z", M)
+        dst = T.cores[(rank + 1 + t) % N]
+        rid, pid = topo.addr(dst, core)
+        mask, ne = topo.mask(core, dst), len(topo.engines(core, dst))
+        sent, came = "sent%d" % t, "came%d" % t
+        waits("G", "net", [qz, sz], [])
+        g.remote_dma(T[lq][:, 0:M].bitcast(dt.uint8), T[qz][:, 0:M].bitcast(dt.uint8), T.sem[came], T.sem[sent], pid, rid, mask)
+        g.remote_dma(T[lp][:, 0:M], T[sz][:, 0:M], T.sem[came], T.sem[sent], pid, rid, mask)
+        count[sent] = 2 * ne
+        back = T.cores[(rank - 1 - t) % N]
+        count[came] = 2 * len(topo.engines(back, core))
+        note("G", "net", came, count[came], [], [lq, lp])
+        copy("V", T.mw[:, 0:C], T.iom[:], ["iom"], ["mw"])
+        tt(T.dl[:], T.lcrow[:, 0:M], T.bigb[:], A.max, ["lcrow", "bigb"], ["dl"])
+        tt(T.lcb[:], T.lbt[:, :, 0:16], T.lbt[:, :, 16:32], A.add, ["lbt"], ["lcb"])
+        for c in range(1, 10):
+            ts(T.cd[:, c, 16:16 + 16 * c], T.lcrow[:, 0:16 * c], T.lcw[:, c:c + 1], A.is_equal, ["lcrow", "lcw"], [("cd", 176 * c + 16, 176 * c + 176)])
+        tt(T.cd[:, :, 0:16], T.lcb[:], T.dl[:], A.is_equal, ["lcb", "dl"], [("cd", 176 * c, 176 * c + 16) for c in range(10)])
+        for c in range(10):
+            n = 16 + 16 * c
+            op("S", lambda e: e.activation(T.junk[:, c % 4, 0:n], T.cd[:, c, 0:n], F.Copy, accum_out=T.dup[:, c:c + 1]), [("cd", 176 * c, 176 * c + 176)], [("junk", c % 4, c % 4 + 1), ("dup", c, c + 1)])
+        wrapped(T.lrow[:], "lrow", 20, "yb", "ybt")
+        tt(T.lw[:], T.ybt[:, :, 0], T.ybt[:, :, 16], A.add, ["ybt"], ["lw"])
+        ts(T.loff[:], T.lw[:], 160.0, A.add, ["lw"], ["loff"])
+
+        def means(b):
+            op("V", lambda e: e.tensor_tensor(T.yt[:, C * b:C * b + C], T.tp[:, C * b:C * b + C].indirect(T.loff[:, 0:20]), X[:, b:1280:4], A.add), ["loff", ("tp", C * b, C * b + C), xc], [("yt", b, b + 1)])
+            copy("S", T.yh[:, 480 * b:480 * b + C], T.yt[:, C * b:C * b + C], [("yt", b, b + 1)], [("yh", 480 * b, 480 * b + C)], 0.5)
+        means(0)
+        means(1)
+        ts(T.dof[:], T.dup[:], 320.0, A.mult, ["dup"], ["dof"], 160.0, A.add)
+        tt(T.dof[:], T.dof[:], T.lcw[:], A.add, ["dof", "lcw"], ["dof"])
+        copy("V", T.doff[:], T.dof[:], ["dof"], ["doff"])
+        op("V", lambda e: e.tensor_copy(T.mw[:, 0:2880].indirect(T.doff[:, 0:10]), T.iok[:]), ["doff", "iok"], ["mw"])
+        wrapped(T.mw[:, 0:C], "mw", 20, "xb", "xbt")
+        tt(T.mwf[:], T.xbt[:, :, 0], T.xbt[:, :, 16], A.add, ["xbt"], ["mwf"])
+        ts(T.moff[:], T.mwf[:], 240.0, A.add, ["mwf"], ["moff"])
+        means(2)
+        means(3)
+        if t == R - 1:
+            ts(T.tt[:], T.lrow[:], 160.0, A.add, ["lrow"], ["tt"])
+            dma("Y", T.ol[:], T.tt[0:128:16, :], ["tt"], [])
+        for b in range(4):
+            bank = ("psD", 512 * b, 512 * b + 512)
+            mm(T.psD[:, 512 * b:512 * b + M], bank, ("wq", "wp"), 128 * b, (lq, lp), M)
+        for b in range(4):
+            bank = ("psD", 512 * b, 512 * b + 512)
+            copy("V" if b % 2 else "S", T.yh[:, 480 * b + C:480 * b + 480], T.psD[:, 512 * b:512 * b + M], [bank], [("yh", 480 * b + C, 480 * b + 480)], 0.03125)
+        for b in range(4):
+            copy("V" if b % 2 else "S", T[xn][:, b:1280:4], T.yh[:, 480 * b:480 * b + 480].indirect(T.moff[:, 0:20]), ["moff", ("yh", 480 * b, 480 * b + 480)], [(xn, b, b + 1)])
+
+    quant("qx", "sx", "x%d" % R, C)
+    mm(T.psA[:, 0:C], "psA", ("qv", "sv"), 0, QX, C)
+    dma("Y", T.oc[:], T.qx[:].bitcast(dt.uint8), ["qx"], [])
+    for k in range(4):
+        dma("S" if k % 2 else "Y", T.osc[4 * k:4 * k + 4, :], T.sx[32 * k:32 * k + 4, :], ["sx"], [])
+    copy("V", T.key[:], T.psA[:, 0:C], ["psA"], ["key"])
+    dma("S", T.y[:], T.key[:], ["key"], [])
+    finish()

@@ -7,9 +7,9 @@ MAGIC = 12582912.0
 BIG = 1.0e29
 NSCAN = 2
 SPEC = """x0 1280 b,x1 1280 b,x2 1280 b,x3 1280 b,uin 512 b,vin 512 b,qx 320 q,sx 320 s,qu 128 q,su 128 s,qu3 384 q,su3 384 s,
-qv 128 q,sv 128 s,wq 512 q,wp 512 s,ct 3584 b,qc 896 q,sc 896 s,ia 320 f,k16 320 f,c8 24 f,pi 4 i,pf 8 f,cj 4 f,ui 24 i,uoff 24 u,
-ident 128 b,gm 8 f,big 320 f,bigb 10x16 b,maskc 24 f,ioj 320 b,iom 320 b,iok 160 b,negj 320 f,r32 20x32 f,rt 20x32 f,w 640 f,
-tt 320 f,ds 20x16 f,cmp 20x336 b,junk 4x336 b,scan 4x168 f,q 20 f,qoff 20 u,qp 20 f,y0 20 f,m0 20 f,dig 80 b,mq 640 b,qm 160 q,
+qv 128 q,sv 128 s,wq 512 q,wp 512 s,ct 3584 b,qc 896 q,sc 896 s,ia 128 f,k16 320 f,c8 24 f,pi 8 i,pf 8 f,cj 4 f,ui 24 i,uoff 24 u,
+ident 128 b,gm 8 f,big 320 f,bigb 10x16 b,maskc 24 f,ioj 320 b,iok 160 b,negj 320 f,r32 20x32 f,rt 20x32 f,w 640 f,
+tt 320 f,cmp 20x336 b,junk 4x336 b,scan 4x168 f,q 20 f,qoff 20 u,qp 20 f,y0 20 f,m0 20 f,dig 80 b,mq 640 b,qm 160 q,
 sm 160 s,orow 320 b,qa 160 f,b1 2x80 f,ss 6x40 f,mn 2x40 f,mx 2x40 f,mn2 40 f,mx2 40 f,ma 20 f,mb 20 f,z0 20 f,woff 20 u,hi 20 f,
 lo 20 f,sp 24 f,spm 3x8 f,s4 3x4 f,s2 3x2 f,v3 4 f,y3 4 f,h3 4 f,l3 4 f,ok 4 f,kr 1280 b,qk 320 q,sk 320 s,key 320 f,cc 1280 b,
 qn 320 q,sn 320 s,rb 20x32 b,rbt 20x32 b,roff 20 u,lrow 320 b,lcrow 320 b,lb 10x32 b,lbt 10x32 b,lcb 10x16 b,lcw 10 f,lcoff 10 u,
@@ -138,83 +138,90 @@ def rank_program(g, core, T, topo):
     iota("ui", T.ui[:, 8:16], [[32, 4], [0, 2]], 0, 0, False)
     iota("ui", T.ui[:, 16:24], [[32, 4], [0, 2]], 16, 0, False)
     iota("pi", T.pi[:, 0:1], [[0, 1]], 0, 1, False)
-    iota("ia", T.ia[:], [[1, 320]], 0, 0)
     iota("k16", T.k16[:], [[0, 20], [1, 16]], 0, 0)
+    iota("ia", T.ia[:], [[1, 128]], 0, 0)
+    iota("ioj", T.ioj[:], [[1, 320]], -160, 0)
     iota("c8", T.c8[:], [[0, 3], [1, 8]], 0, 0)
     iota("cj", T.cj[:, 0:3], [[-128, 3]], 0, -1)
+    iota("dig", T.dig[:], [[0, 80]], 0, 0)
+    iota("sp", T.sp[:], [[0, 24]], 0, 0)
+    iota("kr", T.kr[:], [[0, 1280]], 0, 0)
+    iota("negj", T.negj[:], [[-1, 320]], 0, 0)
+    iota("cc", T.cc[:], [[0, 1280]], 0, 0)
+    iota("iok", T.iok[:], [[1, 160]], 80, 0)
 
     def fill(view, name, v):
         op("V", lambda e: e.memset(view, v), [], [name])
     fill(T.ct[:], "ct", 0.0)
-    fill(T.ct[:, 2560:3072:4], "ct", 8192.0)
-    fill(T.ct[:, 2561:3072:4], "ct", 512.0)
-    fill(T.ct[:, 3072:3584], "ct", 1.0)
-    copy("V", T.uoff[:], T.ui[:], ["ui"], ["uoff"])
     ts(T.pi[:, 1:2], T.pi[:, 0:1], 15, A.bitwise_and, [("pi", 0, 1)], [("pi", 1, 2)])
     ts(T.pi[:, 2:3], T.pi[:, 0:1], 4, A.logical_shift_right, [("pi", 0, 1)], [("pi", 2, 3)])
-    ts(T.pi[:, 3:4], T.pi[:, 2:3], 1, A.bitwise_and, [("pi", 2, 3)], [("pi", 3, 4)])
-    copy("V", T.pf[:, 0:3], T.pi[:, 0:3], ["pi"], [("pf", 0, 3)])
-    copy("V", T.pf[:, 4:5], T.pi[:, 3:4], ["pi"], [("pf", 4, 5)])
-    ts(T.pf[:, 3:4], T.pf[:, 4:5], 0.0, A.is_equal, [("pf", 4, 5)], [("pf", 3, 4)])
-    pcol, kcol, gcol, even, odd = (T.pf[:, i:i + 1] for i in range(5))
+    ts(T.pi[:, 5:6], T.pi[:, 0:1], 31, A.bitwise_and, [("pi", 0, 1)], [("pi", 5, 6)])
+    ts(T.pi[:, 4:5], T.pi[:, 2:3], 1, A.bitwise_and, [("pi", 2, 3)], [("pi", 4, 5)])
+    copy("V", T.pf[:, 0:3], T.pi[:, 0:3], [("pi", 0, 3)], [("pf", 0, 3)])
+    copy("V", T.pf[:, 4:6], T.pi[:, 4:6], [("pi", 4, 6)], [("pf", 4, 6)])
+    ts(T.pf[:, 3:4], T.pf[:, 4:5], 0.0, A.is_equal, [("pf", 4, 6)], [("pf", 3, 4)])
+    pcol, kcol, gcol, even, odd, scol = (T.pf[:, i:i + 1] for i in range(6))
+    copy("V", T.uoff[:], T.ui[:], ["ui"], ["uoff"])
+    ts(T.big[:], T.k16[:], scol, A.is_gt, ["k16", "pf"], ["big"], odd, A.max)
+    ts(T.big[:], T.big[:], -2 * BIG, A.mult, ["big"], ["big"], BIG, A.add)
     quant("qu", "su", "uin", 128)
+    for i in (2, 1, 0):
+        a, z, off = 128 * i, 128 * i + 128, T.uoff[:, 8 * i:8 * i + 8]
+        op("V", lambda e: e.tensor_copy(T.qu3[:, a:z].bitcast(dt.uint32), T.qu[:, 0:128].bitcast(dt.uint32).indirect(off)), ["qu", "uoff"], [("qu3", a, z)])
+        op("S", lambda e: e.activation(T.su3[:, a:z], T.su[:, 0:128].indirect(off), F.Copy), ["su", "uoff"], [("su3", a, z)])
     quant("qx", "sx", "x0", C)
-    for i in range(3):
-        op("V", lambda e: e.tensor_copy(T.qu3[:, 128 * i:128 * i + 128].bitcast(dt.uint32), T.qu[:, 0:128].bitcast(dt.uint32).indirect(T.uoff[:, 8 * i:8 * i + 8])), ["qu", "uoff"], [("qu3", 128 * i, 128 * i + 128)])
-        op("V", lambda e: e.tensor_copy(T.su3[:, 128 * i:128 * i + 128], T.su[:, 0:128].indirect(T.uoff[:, 8 * i:8 * i + 8])), ["su", "uoff"], [("su3", 128 * i, 128 * i + 128)])
-    ts(T.ident[:], T.ia[:, 0:128], pcol, A.is_equal, ["ia", "pf"], ["ident"])
-    for b in range(4):
-        copy("V" if b % 2 else "S", T.ct[:, 512 * b + b:512 * b + 512:4], T.ident[:], ["ident"], [("ct", 512 * b, 512 * b + 512)])
-    ts(T.big[:], T.k16[:], kcol, A.is_ge, ["k16", "pf"], ["big"], 2 * BIG, A.mult)
-    ts(T.big[:], T.big[:], -BIG, A.add, ["big"], ["big"])
+
+    def more_constants():
+        ts(T.ident[:], T.ia[:], pcol, A.is_equal, ["ia", "pf"], ["ident"])
+        for b in range(4):
+            copy("V", T.ct[:, 512 * b + b:512 * b + 512:4], T.ident[:], ["ident"], [("ct", 512 * b, 512 * b + 512)])
+        fill(T.ct[:, 2560:3072:4], ("ct", 2560, 2561), 8192.0)
+        fill(T.ct[:, 2561:3072:4], ("ct", 2561, 2562), 512.0)
+        fill(T.ct[:, 3072:3584], ("ct", 3072, 3584), 1.0)
+        ts(T.ct[:, 2048:2560:4], T.k16[:, 0:128], kcol, A.is_equal, ["k16", "pf"], [("ct", 2048, 2049)], 16.0, A.mult)
+        ts(T.ct[:, 2049:2560:4], T.k16[:, 0:128], kcol, A.is_equal, ["k16", "pf"], [("ct", 2049, 2050)])
 
     def late_constants():
-        ts(T.ct[:, 2048:2560:4], T.k16[:, 0:128], kcol, A.is_equal, ["k16", "pf"], [("ct", 2048, 2560)], 16.0, A.mult)
-        ts(T.ct[:, 2049:2560:4], T.k16[:, 0:128], kcol, A.is_equal, ["k16", "pf"], [("ct", 2048, 2560)])
         quant("qc", "sc", "ct", 512)
         quant("qc", "sc", "ct", 384, 512)
         ts(T.bigb[:], T.k16[:, 0:160], kcol, A.is_ge, ["k16", "pf"], ["bigb"], 2000.0, A.mult)
         ts(T.bigb[:], T.bigb[:], -1000.0, A.add, ["bigb"], ["bigb"])
         ts(T.gm[:], T.ia[:, 0:8], gcol, A.is_equal, ["ia", "pf"], ["gm"])
         ts(T.maskc[:], T.c8[:], gcol, A.is_equal, ["c8", "pf"], ["maskc"])
-        ts(T.ioj[:], T.ia[:], -160.0, A.add, ["ia"], ["ioj"])
-        ts(T.iom[:], T.ia[:], -240.0, A.add, ["ia"], ["iom"])
-        ts(T.iok[:], T.ia[:, 0:160], 80.0, A.add, ["ia"], ["iok"])
-        ts(T.negj[:], T.ia[:], -1.0, A.mult, ["ia"], ["negj"])
-        fill(T.dig[:], "dig", 0.0)
-        fill(T.kr[:], "kr", 0.0)
-        fill(T.cc[:], "cc", 0.0)
-        fill(T.sp[:], "sp", 0.0)
         quant("qv", "sv", "vin", 128)
 
     QC, QU, QX = ("qc", "sc"), ("qu3", "su3"), ("qx", "sx")
 
-    def wrapped(row, rname, n, buf, bt):
-        copy("V", T[buf][:, 0:n, 0:16], row, [rname, "pf"], [(buf, 0, 1)], even)
-        copy("V", T[buf][:, 0:n, 16:32], row, [rname, "pf"], [(buf, 1, 2)], odd)
-        op("V", lambda e: e.transpose(T[bt][:], T[buf][:]), [buf], [bt])
+    def wrapped(qs, row, rname, n, buf, bt):
+        if qs:
+            copy(qs[0], T[buf][:, 0:n, 0:16], row, [rname, "pf"], [(buf, 0, 1)], even)
+            copy(qs[1], T[buf][:, 0:n, 16:32], row, [rname, "pf"], [(buf, 1, 2)], odd)
+        if bt:
+            op("V", lambda e: e.transpose(T[bt][:], T[buf][:]), [buf], [bt])
 
     for t in range(R):
         xc, xn = "x%d" % t, "x%d" % (t + 1)
         X = T[xc]
         if t:
             quant("qx", "sx", xc, C)
+        iota("mw", T.mw[:, 0:C], [[1, C]], -240, 0)
         mm(T.psB[:, 0:C], "psB", QU, 256, QX, C)
         mm(T.psA[:, 0:C], "psA", QU, 128, QX, C)
         mm(T.psS[:, 0:C], "psS", QU, 0, QX, C)
         mm(T.psV[:, 0:C], "psV", QU, 0, QX, C)
-        copy("V", T.r32[:, :, 16:32], T.psB[:, 0:C], ["psB"], [("r32", 1, 2)])
-        copy("S", T.r32[:, :, 0:16], T.psA[:, 0:C], ["psA"], [("r32", 0, 1)])
+        if t == 0:
+            more_constants()
+        tt(T.r32[:, :, 16:32], T.psB[:, 0:C], T.big[:], A.max, ["psB", "big"], [("r32", 1, 2)])
+        tt(T.r32[:, :, 0:16], T.psA[:, 0:C], T.big[:], A.max, ["psA", "big"], [("r32", 0, 1)])
         op("V", lambda e: e.transpose(T.rt[:], T.r32[:]), ["r32"], ["rt"])
         op("S", lambda e: e.activation(T.tt[:], T.psS[:, 0:C], F.Abs, bias=2.0 ** -120, scale=1.25 * 2.0 ** -24), ["psS"], ["tt"])
         copy("S", T.w[:, 0:C], T.psS[:, 0:C], ["psS"], [("w", 0, C)])
-        tt(T.ds[:], T.psV[:, 0:C], T.big[:], A.max, ["psV", "big"], ["ds"])
-        tt(T.cmp[:, :, 0:16], T.rt[:, :, 0:16], T.ds[:], A.is_equal, ["rt", "ds"], ["cmp"])
+        tt(T.cmp[:, :, 0:16], T.rt[:, :, 0:16], T.psV[:, 0:C], A.is_equal, ["rt", "psV"], ["cmp"])
         tt(T.w[:, C:2 * C], T.psV[:, 0:C], T.tt[:], A.add, ["psV", "tt"], [("w", C, 2 * C)])
         ns = 0
         for c in range(20):
             ct = ("cmp", 336 * c, 336 * c + 336)
-            ts(T.cmp[:, c, 16:336], T.w[:, 16 * c:16 * c + C], T.rt[:, c, 0:1], A.is_gt, ["w", "rt"], [ct])
+            ts(T.cmp[:, c, 16:336], T.w[:, 16 * c:16 * c + C], T.rt[:, c, 16:17], A.is_gt, ["w", "rt"], [ct])
             if c >= 20 - NSCAN:
                 op("V", lambda e: e.tensor_tensor_scan(T.scan[:, ns, :], T.cmp[:, c, 0:168], T.cmp[:, c, 168:336], 0.0, A.add, A.add), [ct], [("scan", ns, ns + 1)])
                 ns += 1
@@ -222,8 +229,7 @@ def rank_program(g, core, T, topo):
                 op("S", lambda e: e.activation(T.junk[:, c % 4, :], T.cmp[:, c, :], F.Copy, accum_out=T.q[:, c:c + 1]), [ct], [("junk", c % 4, c % 4 + 1), ("q", c, c + 1)])
         if t == 0:
             late_constants()
-        if ns:
-            copy("V", T.q[:, 20 - ns:20], T.scan[:, 0:ns, 167], ["scan"], [("q", 20 - ns, 20)])
+        copy("V", T.q[:, 20 - ns:20], T.scan[:, 0:ns, 167], ["scan"], [("q", 20 - ns, 20)])
         for b in range(4):
             mm(T.psD[:, 512 * b:512 * b + C], ("psD", 512 * b, 512 * b + 512), QC, 128 * b, QX, C)
         ts(T.y0[:], T.q[:], 0.0625, A.mult, ["q"], ["y0"], MAGIC, A.add)
@@ -231,11 +237,11 @@ def rank_program(g, core, T, topo):
         ts(T.m0[:], T.y0[:], -MAGIC, A.add, ["y0"], ["m0"], -16.0, A.mult)
         tt(T.dig[:, 1:80:4], T.q[:], T.m0[:], A.add, ["q", "m0"], [("dig", 1, 2)])
         for h in range(8):
-            copy("S" if h % 3 == 1 else "V", T.mq[:, 80 * h:80 * h + 80], T.dig[:], ["dig", "gm"], [("mq", h, h + 1)], T.gm[:, h:h + 1])
-        quant("qm", "sm", "mq", M)
-        mm(T.psA[:, 0:M], "psA", QC, 512, ("qm", "sm"), M)
+            copy("S" if h % 2 else "V", T.mq[:, 80 * h:80 * h + 80], T.dig[:], ["dig", "gm"], [("mq", h, h + 1)], T.gm[:, h:h + 1])
         copy("V", T.qoff[:], T.q[:], ["q"], ["qoff"])
         ts(T.qp[:], T.q[:], -160.0, A.add, ["q"], ["qp"])
+        quant("qm", "sm", "mq", M)
+        mm(T.psA[:, 0:M], "psA", QC, 512, ("qm", "sm"), M)
         op("V", lambda e: e.tensor_copy(T.orow[:, 0:C].indirect(T.qoff[:, 0:20]), T.ioj[:]), ["qoff", "ioj"], ["orow"])
         for b in range(4):
             copy("S", T.tp[:, C * b:C * b + C], T.psD[:, 512 * b:512 * b + C], [("psD", 512 * b, 512 * b + 512)], [("tp", C * b, C * b + C)])
@@ -260,15 +266,18 @@ def rank_program(g, core, T, topo):
         tt(T.mx[:, 1, :], T.ss[:, 3:5, 0:20], T.ss[:, 1:3, 20:40], A.max, ["ss"], [("mx", 1, 2)])
         ts(T.y3[:, 0:3], T.v3[:, 0:3], 0.0625, A.mult, ["v3"], ["y3"], MAGIC, A.add)
         tt(T.mn2[:], T.mn[:, 0, :], T.mn[:, 1, :], A.max, ["mn"], ["mn2"])
-        ts(T.h3[:, 0:3], T.y3[:, 0:3], -(MAGIC + 10), A.add, ["y3"], ["h3"])
         ts(T.l3[:, 0:3], T.y3[:, 0:3], -MAGIC, A.add, ["y3"], ["l3"], -16.0, A.mult)
-        tt(T.mx2[:], T.mx[:, 0, :], T.mx[:, 1, :], A.min, ["mx"], ["mx2"])
+        ts(T.h3[:, 0:3], T.y3[:, 0:3], -(MAGIC + 10), A.add, ["y3"], ["h3"])
         tt(T.l3[:, 0:3], T.l3[:, 0:3], T.v3[:, 0:3], A.add, ["l3", "v3"], ["l3"])
-        for e3 in range(3):
+        for d in range(6):
+            e3 = d % 3
             n = min(128, C - 128 * e3)
             a, z = 512 * e3, 512 * e3 + 4 * n
-            copy("V", T.kr[:, a:z:4], T.ident[:, 0:n], ["ident", "h3"], [("kr", 2 * e3, 2 * e3 + 1)], T.h3[:, e3:e3 + 1])
-            copy("S", T.kr[:, a + 1:z:4], T.ident[:, 0:n], ["ident", "l3"], [("kr", 2 * e3 + 1, 2 * e3 + 2)], T.l3[:, e3:e3 + 1])
+            if d < 3:
+                copy("S" if e3 < 2 else "V", T.kr[:, a + 1:z:4], T.ident[:, 0:n], ["ident", "l3"], [("kr", d, d + 1)], T.l3[:, e3:e3 + 1])
+            else:
+                copy("V", T.kr[:, a:z:4], T.ident[:, 0:n], ["ident", "h3"], [("kr", d, d + 1)], T.h3[:, e3:e3 + 1])
+        tt(T.mx2[:], T.mx[:, 0, :], T.mx[:, 1, :], A.min, ["mx"], ["mx2"])
         quant("qk", "sk", "kr", C)
         mm(T.psB[:, 0:C], "psB", QC, 640, ("qk", "sk"), C)
         ts(T.ok[:, 0:3], T.v3[:, 0:3], -160.0, A.add, ["v3"], ["ok"], 512.0, A.mult)
@@ -277,21 +286,22 @@ def rank_program(g, core, T, topo):
         tt(T.ok[:, 0:3], T.ok[:, 0:3], T.cj[:, 0:3], A.add, ["ok", "cj"], ["ok"])
         tt(T.z0[:], T.ma[:], T.mb[:], A.add, ["ma", "mb"], ["z0"])
         tt(T.z0[:], T.z0[:], T.qp[:], A.subtract, ["z0", "qp"], ["z0"])
-        tt(T.key[:], T.psB[:, 0:C], T.negj[:], A.add, ["psB", "negj"], ["key"])
         tt(T.z0[:], T.z0[:], T.mb[:], A.min, ["z0", "mb"], ["z0"])
+        tt(T.z0[:], T.z0[:], T.ma[:], A.max, ["z0", "ma"], ["z0"])
+        tt(T.key[:], T.psB[:, 0:C], T.negj[:], A.add, ["psB", "negj"], ["key"])
         for e3 in range(3):
             ts(T.cc[:, e3:1280:4], T.key[:], T.ok[:, e3:e3 + 1], A.is_lt, ["key", "ok"], [("cc", e3, e3 + 1)])
         quant("qn", "sn", "cc", C)
         mm(T.psS[:, 0:C], "psS", QC, 768, ("qn", "sn"), C)
-        tt(T.z0[:], T.z0[:], T.ma[:], A.max, ["z0", "ma"], ["z0"])
         ts(T.woff[:], T.z0[:], 160.0, A.add, ["z0"], ["woff"])
         op("V", lambda e: e.tensor_copy(T.lrow[:], T.orow[:, 0:C].indirect(T.woff[:, 0:20])), ["woff", "orow"], ["lrow"])
-        ts(T.rb[:, :, 0:16], T.psS[:, 0:C], -160.0, A.add, ["psS"], [("rb", 0, 1)])
-        copy("V", T.rb[:, :, 16:32], T.rb[:, :, 0:16], [("rb", 0, 1)], [("rb", 1, 2)])
+        for h in range(2):
+            op("S", lambda e: e.activation(T.rb[:, :, 16 * h:16 * h + 16], T.psS[:, 0:C], F.Identity, bias=-160.0), ["psS"], [("rb", h, h + 1)])
+        wrapped("SS", T.lrow[:], "lrow", 20, "yb", None)
         op("V", lambda e: e.transpose(T.rbt[:], T.rb[:]), ["rb"], ["rbt"])
         ts(T.roff[:], T.rbt[:, :, 0], 160.0, A.add, ["rbt"], ["roff"])
         op("V", lambda e: e.tensor_copy(T.lcrow[:, 0:C].indirect(T.roff[:, 0:20]), T.lrow[:]), ["roff", "lrow"], ["lcrow"])
-        wrapped(T.lcrow[:, 0:M], "lcrow", 10, "lb", "lbt")
+        wrapped("VV", T.lcrow[:, 0:M], "lcrow", 10, "lb", "lbt")
         tt(T.lcw[:], T.lbt[:, :, 0], T.lbt[:, :, 16], A.add, ["lbt"], ["lcw"])
         ts(T.lcoff[:], T.lcw[:], 160.0, A.add, ["lcw"], ["lcoff"])
         for b in range(4):
@@ -309,35 +319,29 @@ def rank_program(g, core, T, topo):
         back = T.cores[(rank - 1 - t) % N]
         count[came] = 2 * len(topo.engines(back, core))
         note("G", "net", came, count[came], [], [lq, lp])
-        copy("V", T.mw[:, 0:C], T.iom[:], ["iom"], ["mw"])
         tt(T.dl[:], T.lcrow[:, 0:M], T.bigb[:], A.max, ["lcrow", "bigb"], ["dl"])
         tt(T.lcb[:], T.lbt[:, :, 0:16], T.lbt[:, :, 16:32], A.add, ["lbt"], ["lcb"])
-        for c in range(1, 10):
-            ts(T.cd[:, c, 16:16 + 16 * c], T.lcrow[:, 0:16 * c], T.lcw[:, c:c + 1], A.is_equal, ["lcrow", "lcw"], [("cd", 176 * c + 16, 176 * c + 176)])
         tt(T.cd[:, :, 0:16], T.lcb[:], T.dl[:], A.is_equal, ["lcb", "dl"], [("cd", 176 * c, 176 * c + 16) for c in range(10)])
         for c in range(10):
             n = 16 + 16 * c
+            if c:
+                ts(T.cd[:, c, 16:n], T.lcrow[:, 0:16 * c], T.lcw[:, c:c + 1], A.is_equal, ["lcrow", "lcw"], [("cd", 176 * c + 16, 176 * c + 176)])
             op("S", lambda e: e.activation(T.junk[:, c % 4, 0:n], T.cd[:, c, 0:n], F.Copy, accum_out=T.dup[:, c:c + 1]), [("cd", 176 * c, 176 * c + 176)], [("junk", c % 4, c % 4 + 1), ("dup", c, c + 1)])
-        wrapped(T.lrow[:], "lrow", 20, "yb", "ybt")
+        wrapped("", None, "lrow", 20, "yb", "ybt")
         tt(T.lw[:], T.ybt[:, :, 0], T.ybt[:, :, 16], A.add, ["ybt"], ["lw"])
         ts(T.loff[:], T.lw[:], 160.0, A.add, ["lw"], ["loff"])
-
-        def means(b):
+        for b in range(4):
             op("V", lambda e: e.tensor_tensor(T.yt[:, C * b:C * b + C], T.tp[:, C * b:C * b + C].indirect(T.loff[:, 0:20]), X[:, b:1280:4], A.add), ["loff", ("tp", C * b, C * b + C), xc], [("yt", b, b + 1)])
             copy("S", T.yh[:, 480 * b:480 * b + C], T.yt[:, C * b:C * b + C], [("yt", b, b + 1)], [("yh", 480 * b, 480 * b + C)], 0.5)
-        means(0)
-        means(1)
         ts(T.dof[:], T.dup[:], 320.0, A.mult, ["dup"], ["dof"], 160.0, A.add)
         tt(T.dof[:], T.dof[:], T.lcw[:], A.add, ["dof", "lcw"], ["dof"])
         copy("V", T.doff[:], T.dof[:], ["dof"], ["doff"])
         op("V", lambda e: e.tensor_copy(T.mw[:, 0:2880].indirect(T.doff[:, 0:10]), T.iok[:]), ["doff", "iok"], ["mw"])
-        wrapped(T.mw[:, 0:C], "mw", 20, "xb", "xbt")
+        wrapped("VS", T.mw[:, 0:C], "mw", 20, "xb", "xbt")
         tt(T.mwf[:], T.xbt[:, :, 0], T.xbt[:, :, 16], A.add, ["xbt"], ["mwf"])
         ts(T.moff[:], T.mwf[:], 240.0, A.add, ["mwf"], ["moff"])
-        means(2)
-        means(3)
         if t == R - 1:
-            ts(T.tt[:], T.lrow[:], 160.0, A.add, ["lrow"], ["tt"])
+            op("S", lambda e: e.activation(T.tt[:], T.lrow[:], F.Identity, bias=160.0), ["lrow"], ["tt"])
             dma("Y", T.ol[:], T.tt[0:128:16, :], ["tt"], [])
         for b in range(4):
             bank = ("psD", 512 * b, 512 * b + 512)
@@ -351,8 +355,8 @@ def rank_program(g, core, T, topo):
     quant("qx", "sx", "x%d" % R, C)
     mm(T.psA[:, 0:C], "psA", ("qv", "sv"), 0, QX, C)
     dma("Y", T.oc[:], T.qx[:].bitcast(dt.uint8), ["qx"], [])
+    copy("V", T.key[:], T.psA[:, 0:C], ["psA"], ["key"])
     for k in range(4):
         dma("S" if k % 2 else "Y", T.osc[4 * k:4 * k + 4, :], T.sx[32 * k:32 * k + 4, :], ["sx"], [])
-    copy("V", T.key[:], T.psA[:, 0:C], ["psA"], ["key"])
     dma("S", T.y[:], T.key[:], ["key"], [])
     finish()

@@ -5,12 +5,12 @@ F = ActivationFunctionType
 C, M, R = 320, 160, 3
 MAGIC = 12582912.0
 BIG = 1.0e29
-NSCAN = 2
+NS = 8
 SPEC = """x0 1280 b,x1 1280 b,x2 1280 b,x3 1280 b,uin 512 b,vin 512 b,qx 320 q,sx 320 s,qu 128 q,su 128 s,qu3 384 q,su3 384 s,
 qv 128 q,sv 128 s,wq 512 q,wp 512 s,ct 3584 b,qc 896 q,sc 896 s,ia 128 f,k16 320 f,c8 24 f,pi 8 i,pf 8 f,cj 4 f,ui 24 i,uoff 24 u,
-ident 128 b,gm 8 f,big 320 f,bigb 10x16 b,maskc 24 f,ioj 320 b,iok 160 b,negj 320 f,r32 20x32 f,rt 20x32 f,w 640 f,
-tt 320 f,cmp 20x336 b,junk 4x336 b,scan 4x168 f,q 20 f,qoff 20 u,qp 20 f,y0 20 f,m0 20 f,dig 80 b,mq 640 b,qm 160 q,
-sm 160 s,orow 320 b,qa 160 f,b1 2x80 f,ss 6x40 f,mn 2x40 f,mx 2x40 f,mn2 40 f,mx2 40 f,ma 20 f,mb 20 f,z0 20 f,woff 20 u,hi 20 f,
+ident 128 b,gm 8 f,big 320 f,bigb 10x16 b,maskc 24 f,ioj 320 b,iok 160 b,negj 320 f,r32 20x32 f,rt 20x32 f,w 640 f,neg 20 f,
+tt 320 f,cmp 20x336 b,junk 4x336 b,scan 20x168 b,q 20 f,qoff 20 u,qp 20 f,y0 20 f,m0 20 f,dig 80 b,mq 640 b,qm 160 q,
+sm 160 s,orow 320 b,qa 80 f,b1 2x80 f,ss 6x40 f,mn 2x40 f,mx 2x40 f,mn2 40 f,mx2 40 f,ma 20 f,mb 20 f,z0 20 f,woff 20 u,hi 20 f,
 lo 20 f,sp 24 f,spm 3x8 f,s4 3x4 f,s2 3x2 f,v3 4 f,y3 4 f,h3 4 f,l3 4 f,ok 4 f,kr 1280 b,qk 320 q,sk 320 s,key 320 f,cc 1280 b,
 qn 320 q,sn 320 s,rb 20x32 b,rbt 20x32 b,roff 20 u,lrow 320 b,lcrow 320 b,lb 10x32 b,lbt 10x32 b,lcb 10x16 b,lcw 10 f,lcoff 10 u,
 tp 1280 b,z 640 b,yb 20x32 b,ybt 20x32 b,lw 20 f,loff 20 u,dl 10x16 b,cd 10x176 b,dup 10 f,dof 10 f,doff 10 u,mw 2880 b,xb 20x32 b,
@@ -62,7 +62,7 @@ def tracker(g, T):
                 learn(q, sem, val)
 
     def note(q, who, sem, val, reads, writes):
-        hist[(sem, val)] = dict(known[q])
+        hist[(sem, val)] = dict(known[q]) if q else {}
         for toks, wr in ((reads, False), (writes, True)):
             for name, lo, hi in map(token, toks):
                 acc.setdefault(name, []).append((who, sem, val, lo, hi, wr))
@@ -162,16 +162,17 @@ def rank_program(g, core, T, topo):
     ts(T.pf[:, 3:4], T.pf[:, 4:5], 0.0, A.is_equal, [("pf", 4, 6)], [("pf", 3, 4)])
     pcol, kcol, gcol, even, odd, scol = (T.pf[:, i:i + 1] for i in range(6))
     copy("V", T.uoff[:], T.ui[:], ["ui"], ["uoff"])
-    ts(T.big[:], T.k16[:], scol, A.is_gt, ["k16", "pf"], ["big"], odd, A.max)
-    ts(T.big[:], T.big[:], -2 * BIG, A.mult, ["big"], ["big"], BIG, A.add)
     quant("qu", "su", "uin", 128)
     for i in (2, 1, 0):
         a, z, off = 128 * i, 128 * i + 128, T.uoff[:, 8 * i:8 * i + 8]
         op("V", lambda e: e.tensor_copy(T.qu3[:, a:z].bitcast(dt.uint32), T.qu[:, 0:128].bitcast(dt.uint32).indirect(off)), ["qu", "uoff"], [("qu3", a, z)])
         op("S", lambda e: e.activation(T.su3[:, a:z], T.su[:, 0:128].indirect(off), F.Copy), ["su", "uoff"], [("su3", a, z)])
-    quant("qx", "sx", "x0", C)
+        if i == 2:
+            quant("qx", "sx", "x0", C)
+    ts(T.big[:], T.k16[:], scol, A.is_gt, ["k16", "pf"], ["big"], odd, A.max)
+    ts(T.big[:], T.big[:], -2 * BIG, A.mult, ["big"], ["big"], BIG, A.add)
 
-    def more_constants():
+    def late_constants():
         ts(T.ident[:], T.ia[:], pcol, A.is_equal, ["ia", "pf"], ["ident"])
         for b in range(4):
             copy("V", T.ct[:, 512 * b + b:512 * b + 512:4], T.ident[:], ["ident"], [("ct", 512 * b, 512 * b + 512)])
@@ -180,8 +181,6 @@ def rank_program(g, core, T, topo):
         fill(T.ct[:, 3072:3584], ("ct", 3072, 3584), 1.0)
         ts(T.ct[:, 2048:2560:4], T.k16[:, 0:128], kcol, A.is_equal, ["k16", "pf"], [("ct", 2048, 2049)], 16.0, A.mult)
         ts(T.ct[:, 2049:2560:4], T.k16[:, 0:128], kcol, A.is_equal, ["k16", "pf"], [("ct", 2049, 2050)])
-
-    def late_constants():
         quant("qc", "sc", "ct", 512)
         quant("qc", "sc", "ct", 384, 512)
         ts(T.bigb[:], T.k16[:, 0:160], kcol, A.is_ge, ["k16", "pf"], ["bigb"], 2000.0, A.mult)
@@ -190,7 +189,7 @@ def rank_program(g, core, T, topo):
         ts(T.maskc[:], T.c8[:], gcol, A.is_equal, ["c8", "pf"], ["maskc"])
         quant("qv", "sv", "vin", 128)
 
-    QC, QU, QX = ("qc", "sc"), ("qu3", "su3"), ("qx", "sx")
+    QC, QX = ("qc", "sc"), ("qx", "sx")
 
     def wrapped(qs, row, rname, n, buf, bt):
         if qs:
@@ -205,49 +204,52 @@ def rank_program(g, core, T, topo):
         if t:
             quant("qx", "sx", xc, C)
         iota("mw", T.mw[:, 0:C], [[1, C]], -240, 0)
-        mm(T.psB[:, 0:C], "psB", QU, 256, QX, C)
-        mm(T.psA[:, 0:C], "psA", QU, 128, QX, C)
-        mm(T.psS[:, 0:C], "psS", QU, 0, QX, C)
-        mm(T.psV[:, 0:C], "psV", QU, 0, QX, C)
-        if t == 0:
-            more_constants()
+        for bank, s0 in (("psB", 256), ("psA", 128), ("psS", 0), ("psV", 0)):
+            op("T", lambda e: e.matmul_mx(T[bank][:, 0:C], T.qu3[:, s0:s0 + 128], T.su3[:, s0:s0 + 128], T.qx[:, 0:C], T.sx[:, 0:C], True, True),
+               [("qu3", s0, s0 + 128), ("su3", s0, s0 + 128), "qx", "sx"], [bank])
         tt(T.r32[:, :, 16:32], T.psB[:, 0:C], T.big[:], A.max, ["psB", "big"], [("r32", 1, 2)])
         tt(T.r32[:, :, 0:16], T.psA[:, 0:C], T.big[:], A.max, ["psA", "big"], [("r32", 0, 1)])
         op("V", lambda e: e.transpose(T.rt[:], T.r32[:]), ["r32"], ["rt"])
         op("S", lambda e: e.activation(T.tt[:], T.psS[:, 0:C], F.Abs, bias=2.0 ** -120, scale=1.25 * 2.0 ** -24), ["psS"], ["tt"])
         copy("S", T.w[:, 0:C], T.psS[:, 0:C], ["psS"], [("w", 0, C)])
-        tt(T.cmp[:, :, 0:16], T.rt[:, :, 0:16], T.psV[:, 0:C], A.is_equal, ["rt", "psV"], ["cmp"])
+        ts(T.neg[:], T.rt[:, :, 16], -1.0, A.mult, ["rt"], ["neg"])
         tt(T.w[:, C:2 * C], T.psV[:, 0:C], T.tt[:], A.add, ["psV", "tt"], [("w", C, 2 * C)])
-        ns = 0
-        for c in range(20):
-            ct = ("cmp", 336 * c, 336 * c + 336)
-            ts(T.cmp[:, c, 16:336], T.w[:, 16 * c:16 * c + C], T.rt[:, c, 16:17], A.is_gt, ["w", "rt"], [ct])
-            if c >= 20 - NSCAN:
-                op("V", lambda e: e.tensor_tensor_scan(T.scan[:, ns, :], T.cmp[:, c, 0:168], T.cmp[:, c, 168:336], 0.0, A.add, A.add), [ct], [("scan", ns, ns + 1)])
-                ns += 1
-            else:
-                op("S", lambda e: e.activation(T.junk[:, c % 4, :], T.cmp[:, c, :], F.Copy, accum_out=T.q[:, c:c + 1]), [ct], [("junk", c % 4, c % 4 + 1), ("q", c, c + 1)])
+        tt(T.cmp[:, :, 0:16], T.rt[:, :, 0:16], T.psV[:, 0:C], A.is_equal, ["rt", "psV"], [("cmp", 336 * c, 336 * c + 16) for c in range(20)])
+        for c in range(NS):
+            lo, hi = 336 * c, 336 * c + 336
+            op("S", lambda e: e.activation(T.cmp[:, c, 16:336], T.w[:, 16 * c:16 * c + C], F.Sign, bias=T.neg[:, c:c + 1]), ["w", "neg"], [("cmp", lo + 16, hi)])
+            if c:
+                op("S", lambda e: e.activation(T.junk[:, c % 4, :], T.cmp[:, c - 1, :], F.Relu, accum_out=T.q[:, c - 1:c]), [("cmp", lo - 336, lo)], [("junk", c % 4, c % 4 + 1), ("q", c - 1, c)])
+        op("S", lambda e: e.activation(T.junk[:, 0, :], T.cmp[:, NS - 1, :], F.Relu, accum_out=T.q[:, NS - 1:NS]), [("cmp", 336 * NS - 336, 336 * NS)], [("junk", 0, 1), ("q", NS - 1, NS)])
+
+        def total(c):
+            op("V", lambda e: e.tensor_tensor_scan(T.scan[:, c, :], T.cmp[:, c, 0:168], T.cmp[:, c, 168:336], -160.0, A.add, A.add), [("cmp", 336 * c, 336 * c + 336)], [("scan", c, c + 1)])
+        for c in range(NS, 20):
+            ts(T.cmp[:, c, 16:336], T.w[:, 16 * c:16 * c + C], T.rt[:, c, 16:17], A.is_gt, ["w", "rt"], [("cmp", 336 * c + 16, 336 * c + 336)])
+            if c > NS:
+                total(c - 1)
+        total(19)
         if t == 0:
             late_constants()
-        copy("V", T.q[:, 20 - ns:20], T.scan[:, 0:ns, 167], ["scan"], [("q", 20 - ns, 20)])
+        ts(T.q[:, NS:20], T.scan[:, NS:20, 167], 160.0, A.add, ["scan"], [("q", NS, 20)])
         for b in range(4):
             mm(T.psD[:, 512 * b:512 * b + C], ("psD", 512 * b, 512 * b + 512), QC, 128 * b, QX, C)
         ts(T.y0[:], T.q[:], 0.0625, A.mult, ["q"], ["y0"], MAGIC, A.add)
-        ts(T.dig[:, 0:80:4], T.y0[:], -(MAGIC + 10), A.add, ["y0"], [("dig", 0, 1)])
+        copy("V", T.qoff[:], T.q[:], ["q"], ["qoff"])
         ts(T.m0[:], T.y0[:], -MAGIC, A.add, ["y0"], ["m0"], -16.0, A.mult)
+        ts(T.dig[:, 0:80:4], T.y0[:], -(MAGIC + 10), A.add, ["y0"], [("dig", 0, 1)])
         tt(T.dig[:, 1:80:4], T.q[:], T.m0[:], A.add, ["q", "m0"], [("dig", 1, 2)])
         for h in range(8):
-            copy("S" if h % 2 else "V", T.mq[:, 80 * h:80 * h + 80], T.dig[:], ["dig", "gm"], [("mq", h, h + 1)], T.gm[:, h:h + 1])
-        copy("V", T.qoff[:], T.q[:], ["q"], ["qoff"])
+            copy("S" if h in (1, 3, 5) else "V", T.mq[:, 80 * h:80 * h + 80], T.dig[:], ["dig", "gm"], [("mq", h, h + 1)], T.gm[:, h:h + 1])
         ts(T.qp[:], T.q[:], -160.0, A.add, ["q"], ["qp"])
         quant("qm", "sm", "mq", M)
         mm(T.psA[:, 0:M], "psA", QC, 512, ("qm", "sm"), M)
         op("V", lambda e: e.tensor_copy(T.orow[:, 0:C].indirect(T.qoff[:, 0:20]), T.ioj[:]), ["qoff", "ioj"], ["orow"])
         for b in range(4):
             copy("S", T.tp[:, C * b:C * b + C], T.psD[:, 512 * b:512 * b + C], [("psD", 512 * b, 512 * b + 512)], [("tp", C * b, C * b + C)])
-        copy("V", T.qa[:], T.psA[:, 0:M], ["psA"], ["qa"])
-        tt(T.b1[:, 0, :], T.qa[:, 0:80], T.qa[:, 80:160], A.min, ["qa"], [("b1", 0, 1)])
-        tt(T.b1[:, 1, :], T.qa[:, 0:80], T.qa[:, 80:160], A.max, ["qa"], [("b1", 1, 2)])
+        copy("V", T.qa[:], T.psA[:, 80:160], ["psA"], ["qa"])
+        tt(T.b1[:, 0, :], T.psA[:, 0:80], T.qa[:], A.min, ["psA", "qa"], [("b1", 0, 1)])
+        tt(T.b1[:, 1, :], T.psA[:, 0:80], T.qa[:], A.max, ["psA", "qa"], [("b1", 1, 2)])
         tt(T.ss[:, 0:4:3, :], T.b1[:, :, 0:40], T.b1[:, :, 40:80], A.max, ["b1"], [("ss", 0, 1), ("ss", 3, 4)])
         tt(T.ss[:, 1:6:4, :], T.b1[:, :, 0:40], T.b1[:, :, 40:80], A.min, ["b1"], [("ss", 1, 2), ("ss", 5, 6)])
         s = lambda i: ("ss", i, i + 1)
@@ -272,15 +274,13 @@ def rank_program(g, core, T, topo):
         for d in range(6):
             e3 = d % 3
             n = min(128, C - 128 * e3)
-            a, z = 512 * e3, 512 * e3 + 4 * n
-            if d < 3:
-                copy("S" if e3 < 2 else "V", T.kr[:, a + 1:z:4], T.ident[:, 0:n], ["ident", "l3"], [("kr", d, d + 1)], T.l3[:, e3:e3 + 1])
-            else:
-                copy("V", T.kr[:, a:z:4], T.ident[:, 0:n], ["ident", "h3"], [("kr", d, d + 1)], T.h3[:, e3:e3 + 1])
-        tt(T.mx2[:], T.mx[:, 0, :], T.mx[:, 1, :], A.min, ["mx"], ["mx2"])
+            a, z = 512 * e3 + d // 3, 512 * e3 + 4 * n
+            src = "l3" if d > 2 else "h3"
+            copy("V", T.kr[:, a:z:4], T.ident[:, 0:n], ["ident", src], [("kr", d, d + 1)], T[src][:, e3:e3 + 1])
         quant("qk", "sk", "kr", C)
         mm(T.psB[:, 0:C], "psB", QC, 640, ("qk", "sk"), C)
         ts(T.ok[:, 0:3], T.v3[:, 0:3], -160.0, A.add, ["v3"], ["ok"], 512.0, A.mult)
+        tt(T.mx2[:], T.mx[:, 0, :], T.mx[:, 1, :], A.min, ["mx"], ["mx2"])
         tt(T.ma[:], T.mn2[:, 0:20], T.mn2[:, 20:40], A.max, ["mn2"], ["ma"])
         tt(T.mb[:], T.mx2[:, 0:20], T.mx2[:, 20:40], A.min, ["mx2"], ["mb"])
         tt(T.ok[:, 0:3], T.ok[:, 0:3], T.cj[:, 0:3], A.add, ["ok", "cj"], ["ok"])
@@ -288,15 +288,15 @@ def rank_program(g, core, T, topo):
         tt(T.z0[:], T.z0[:], T.qp[:], A.subtract, ["z0", "qp"], ["z0"])
         tt(T.z0[:], T.z0[:], T.mb[:], A.min, ["z0", "mb"], ["z0"])
         tt(T.z0[:], T.z0[:], T.ma[:], A.max, ["z0", "ma"], ["z0"])
+        ts(T.woff[:], T.z0[:], 160.0, A.add, ["z0"], ["woff"])
         tt(T.key[:], T.psB[:, 0:C], T.negj[:], A.add, ["psB", "negj"], ["key"])
         for e3 in range(3):
             ts(T.cc[:, e3:1280:4], T.key[:], T.ok[:, e3:e3 + 1], A.is_lt, ["key", "ok"], [("cc", e3, e3 + 1)])
         quant("qn", "sn", "cc", C)
         mm(T.psS[:, 0:C], "psS", QC, 768, ("qn", "sn"), C)
-        ts(T.woff[:], T.z0[:], 160.0, A.add, ["z0"], ["woff"])
         op("V", lambda e: e.tensor_copy(T.lrow[:], T.orow[:, 0:C].indirect(T.woff[:, 0:20])), ["woff", "orow"], ["lrow"])
-        for h in range(2):
-            op("S", lambda e: e.activation(T.rb[:, :, 16 * h:16 * h + 16], T.psS[:, 0:C], F.Identity, bias=-160.0), ["psS"], [("rb", h, h + 1)])
+        ts(T.rb[:, :, 0:16], T.psS[:, 0:C], -160.0, A.add, ["psS"], [("rb", 0, 1)])
+        copy("V", T.rb[:, :, 16:32], T.rb[:, :, 0:16], [("rb", 0, 1)], [("rb", 1, 2)])
         wrapped("SS", T.lrow[:], "lrow", 20, "yb", None)
         op("V", lambda e: e.transpose(T.rbt[:], T.rb[:]), ["rb"], ["rbt"])
         ts(T.roff[:], T.rbt[:, :, 0], 160.0, A.add, ["rbt"], ["roff"])
@@ -306,6 +306,7 @@ def rank_program(g, core, T, topo):
         ts(T.lcoff[:], T.lcw[:], 160.0, A.add, ["lcw"], ["lcoff"])
         for b in range(4):
             copy("V" if b % 2 else "S", T.z[:, b:640:4], T.tp[:, C * b:C * b + C].indirect(T.lcoff[:, 0:10]), ["lcoff", ("tp", C * b, C * b + C)], [("z", b, b + 1)])
+        tt(T.dl[:], T.lcrow[:, 0:M], T.bigb[:], A.max, ["lcrow", "bigb"], ["dl"])
         qz, sz, lq, lp = "qz%d" % t, "sz%d" % t, "lq%d" % t, "ls%d" % t
         quant(qz, sz, "z", M)
         dst = T.cores[(rank + 1 + t) % N]
@@ -318,26 +319,24 @@ def rank_program(g, core, T, topo):
         count[sent] = 2 * ne
         back = T.cores[(rank - 1 - t) % N]
         count[came] = 2 * len(topo.engines(back, core))
-        note("G", "net", came, count[came], [], [lq, lp])
-        tt(T.dl[:], T.lcrow[:, 0:M], T.bigb[:], A.max, ["lcrow", "bigb"], ["dl"])
+        note(None, "net", came, count[came], [], [lq, lp])
         tt(T.lcb[:], T.lbt[:, :, 0:16], T.lbt[:, :, 16:32], A.add, ["lbt"], ["lcb"])
         tt(T.cd[:, :, 0:16], T.lcb[:], T.dl[:], A.is_equal, ["lcb", "dl"], [("cd", 176 * c, 176 * c + 16) for c in range(10)])
         for c in range(10):
             n = 16 + 16 * c
             if c:
                 ts(T.cd[:, c, 16:n], T.lcrow[:, 0:16 * c], T.lcw[:, c:c + 1], A.is_equal, ["lcrow", "lcw"], [("cd", 176 * c + 16, 176 * c + 176)])
-            op("S", lambda e: e.activation(T.junk[:, c % 4, 0:n], T.cd[:, c, 0:n], F.Copy, accum_out=T.dup[:, c:c + 1]), [("cd", 176 * c, 176 * c + 176)], [("junk", c % 4, c % 4 + 1), ("dup", c, c + 1)])
+            op("S", lambda e: e.activation(T.junk[:, c % 4, 0:n], T.cd[:, c, 0:n], F.Copy, scale=320.0, accum_out=T.dup[:, c:c + 1]), [("cd", 176 * c, 176 * c + 176)], [("junk", c % 4, c % 4 + 1), ("dup", c, c + 1)])
         wrapped("", None, "lrow", 20, "yb", "ybt")
         tt(T.lw[:], T.ybt[:, :, 0], T.ybt[:, :, 16], A.add, ["ybt"], ["lw"])
         ts(T.loff[:], T.lw[:], 160.0, A.add, ["lw"], ["loff"])
         for b in range(4):
             op("V", lambda e: e.tensor_tensor(T.yt[:, C * b:C * b + C], T.tp[:, C * b:C * b + C].indirect(T.loff[:, 0:20]), X[:, b:1280:4], A.add), ["loff", ("tp", C * b, C * b + C), xc], [("yt", b, b + 1)])
             copy("S", T.yh[:, 480 * b:480 * b + C], T.yt[:, C * b:C * b + C], [("yt", b, b + 1)], [("yh", 480 * b, 480 * b + C)], 0.5)
-        ts(T.dof[:], T.dup[:], 320.0, A.mult, ["dup"], ["dof"], 160.0, A.add)
-        tt(T.dof[:], T.dof[:], T.lcw[:], A.add, ["dof", "lcw"], ["dof"])
-        copy("V", T.doff[:], T.dof[:], ["dof"], ["doff"])
+        tt(T.dof[:], T.dup[:], T.lcw[:], A.add, ["dup", "lcw"], ["dof"])
+        ts(T.doff[:], T.dof[:], 160.0, A.add, ["dof"], ["doff"])
         op("V", lambda e: e.tensor_copy(T.mw[:, 0:2880].indirect(T.doff[:, 0:10]), T.iok[:]), ["doff", "iok"], ["mw"])
-        wrapped("VS", T.mw[:, 0:C], "mw", 20, "xb", "xbt")
+        wrapped("VV", T.mw[:, 0:C], "mw", 20, "xb", "xbt")
         tt(T.mwf[:], T.xbt[:, :, 0], T.xbt[:, :, 16], A.add, ["xbt"], ["mwf"])
         ts(T.moff[:], T.mwf[:], 240.0, A.add, ["mwf"], ["moff"])
         if t == R - 1:

from concourse.mybir import dt, AluOpType, ActivationFunctionType

A = AluOpType
F = ActivationFunctionType
C, M, R = 320, 160, 3
MAGIC = 12582912.0
BIG = 1.0e29
NS = 8
SPEC = """x0 1280 b,x1 1280 b,x2 1280 b,x3 1280 b,uin 512 b,vin 512 b,qx 320 q,sx 320 s,qu 128 q,su 128 s,qu3 384 q,su3 384 s,
qv 128 q,sv 128 s,wq 512 q,wp 512 s,ct 3584 b,qc 896 q,sc 896 s,ia 128 f,k16 320 f,c8 24 f,pi 8 i,pf 8 f,cj 4 f,ui 24 i,uoff 24 u,
ident 128 b,gm 8 f,big 320 f,bigb 10x16 b,maskc 24 f,ioj 320 b,iok 160 b,negj 320 f,r32 20x32 f,rt 20x32 f,w 640 f,neg 20 f,
tt 320 f,cmp 20x336 b,junk 4x336 b,scan 20x168 b,q 20 f,qoff 20 u,qp 20 f,y0 20 f,m0 20 f,dig 80 b,mq 640 b,qm 160 q,
sm 160 s,orow 320 b,qa 80 f,b1 2x80 f,ss 6x40 f,mn 2x40 f,mx 2x40 f,mn2 40 f,mx2 40 f,ma 20 f,mb 20 f,z0 20 f,woff 20 u,hi 20 f,
lo 20 f,sp 24 f,spm 3x8 f,s4 3x4 f,s2 3x2 f,v3 4 f,y3 4 f,h3 4 f,l3 4 f,ok 4 f,kr 1280 b,qk 320 q,sk 320 s,key 320 f,cc 1280 b,
qn 320 q,sn 320 s,rb 20x32 b,rbt 20x32 b,roff 20 u,lrow 320 b,lcrow 320 b,lb 10x32 b,lbt 10x32 b,lcb 10x16 b,lcw 10 f,lcoff 10 u,
tp 1280 b,z 640 b,yb 20x32 b,ybt 20x32 b,lw 20 f,loff 20 u,dl 10x16 b,cd 10x176 b,dup 10 f,dof 10 f,doff 10 u,mw 2880 b,xb 20x32 b,
xbt 20x32 b,mwf 20 f,moff 20 u,yt 1280 f,yh 1920 b,qz0 160 q,sz0 160 s,lq0 160 q,ls0 160 s,qz1 160 q,sz1 160 s,lq1 160 q,ls1 160 s,
qz2 160 q,sz2 160 s,lq2 160 q,ls2 160 s"""
KIND = {"b": "bfloat16", "f": "float32", "i": "int32", "u": "uint16", "q": "float8_e4m3fn_x4", "s": "uint8"}
SCRATCH = {}
for _e in SPEC.replace("\n", "").split(","):
    _n, _s, _k = _e.split()
    SCRATCH[_n] = ("sbuf", [128] + [int(v) for v in _s.split("x")], KIND[_k])
for _n in ("psA", "psB", "psS", "psV"):
    SCRATCH[_n] = ("psum", [128, 512], "float32")
SCRATCH["psD"] = ("psum", [128, 2048], "float32")
SEMAPHORES = ["eV", "eS", "eT", "eG"] + ["d%d" % i for i in range(16)] + ["sent%d" % t for t in range(R)] + ["came%d" % t for t in range(R)]


def tracker(g, T):
    queue = {"V": g.vector, "S": g.scalar, "T": g.tensor, "G": g, "Y": g.sync}
    count, acc, known, hist, ndma = {}, {}, {q: {} for q in queue}, {}, [0]

    def token(x):
        return (x, 0, 1 << 30) if isinstance(x, str) else x

    def learn(q, sem, val):
        k = known[q]
        if k.get(sem, 0) < val:
            k[sem] = val
        for s, v in hist.get((sem, val), {}).items():
            if k.get(s, 0) < v:
                k[s] = v

    def waits(q, who, reads, writes):
        req = {}
        for toks, wr in ((reads, False), (writes, True)):
            for name, lo, hi in map(token, toks):
                for owner, sem, val, alo, ahi, aw in acc.get(name, ()):
                    if alo >= hi or lo >= ahi:
                        continue
                    if not (aw or wr) and not (name.startswith("ps") and owner != who):
                        continue
                    if wr and not aw and owner == who:
                        continue
                    if who == "T" and owner == "T":
                        continue
                    req[sem] = max(req.get(sem, 0), val)
        for sem, val in sorted(req.items(), key=lambda e: e[0]):
            if known[q].get(sem, 0) < val:
                queue[q].wait_ge(T.sem[sem], val)
                learn(q, sem, val)

    def note(q, who, sem, val, reads, writes):
        hist[(sem, val)] = dict(known[q]) if q else {}
        for toks, wr in ((reads, False), (writes, True)):
            for name, lo, hi in map(token, toks):
                acc.setdefault(name, []).append((who, sem, val, lo, hi, wr))

    def op(q, fn, reads, writes):
        waits(q, q, reads, writes)
        sem = "e" + q
        count[sem] = count.get(sem, 0) + 1
        fn(queue[q]).then_inc(T.sem[sem], 1)
        note(q, q, sem, count[sem], reads, writes)

    def dma(q, out, in_, reads, writes):
        sem = "d%d" % ndma[0]
        ndma[0] += 1
        waits(q, sem, reads, writes)
        queue[q].dma_start(out, in_).then_inc(T.sem[sem], 16)
        count[sem] = 16
        note(q, sem, sem, 16, reads, writes)

    def finish():
        for sem in sorted(count):
            g.wait_ge(T.sem[sem], count[sem])
    return op, dma, waits, note, count, finish


def rank_program(g, core, T, topo):
    rank = T.rank_of(core)
    if rank is None:
        return
    N = len(T.cores)
    op, dma, waits, note, count, finish = tracker(g, T)

    def copy(q, out, in_, rd, wr, scale=None):
        if q == "S":
            if scale is None:
                op(q, lambda e: e.activation(out, in_, F.Copy), rd, wr)
            else:
                op(q, lambda e: e.activation(out, in_, F.Copy, scale=scale), rd, wr)
        elif scale is None:
            op(q, lambda e: e.tensor_copy(out, in_), rd, wr)
        else:
            op(q, lambda e: e.tensor_scalar(out, in_, scale, None, A.mult), rd, wr)

    def ts(out, in_, s1, o1, rd, wr, s2=None, o2=None):
        if o2 is None:
            op("V", lambda e: e.tensor_scalar(out, in_, s1, None, o1), rd, wr)
        else:
            op("V", lambda e: e.tensor_scalar(out, in_, s1, s2, o1, o2), rd, wr)

    def tt(out, a, b, o, rd, wr):
        op("V", lambda e: e.tensor_tensor(out, a, b, o), rd, wr)

    def quant(qn, sn, tn, n, q0=0):
        op("V", lambda e: e.quantize_mx(T[qn][:, q0:q0 + n], T[sn][:, q0:q0 + n], T[tn][:, 4 * q0:4 * (q0 + n)]), [tn], [qn, sn])

    def mm(out, otok, st, s0, mv, n):
        lq, lp, rq, rp = T[st[0]], T[st[1]], T[mv[0]], T[mv[1]]
        op("T", lambda e: e.matmul_mx(out, lq[:, s0:s0 + 128], lp[:, s0:s0 + 128], rq[:, 0:n], rp[:, 0:n], True, True),
           [st[0], st[1], mv[0], mv[1]], [otok])

    dma("Y", T.x0[:], T.x[:], [], ["x0"])
    dma("S", T.uin[:], T.u[:], [], ["uin"])
    dma("Y", T.wq[:].bitcast(dt.uint8), T.wc[:], [], ["wq"])
    dma("S", T.wp[:], T.ws[:], [], ["wp"])
    dma("Y", T.vin[:], T.v[:], [], ["vin"])

    def iota(name, view, pat, base, cm, f=True):
        if f:
            op("G", lambda e: e.iota(view, pat, base, cm, allow_small_or_imprecise_dtypes=True), [], [name])
        else:
            op("G", lambda e: e.iota(view, pat, base, cm), [], [name])
    iota("ui", T.ui[:, 0:8], [[16, 8]], 0, 0, False)
    iota("ui", T.ui[:, 8:16], [[32, 4], [0, 2]], 0, 0, False)
    iota("ui", T.ui[:, 16:24], [[32, 4], [0, 2]], 16, 0, False)
    iota("pi", T.pi[:, 0:1], [[0, 1]], 0, 1, False)
    iota("k16", T.k16[:], [[0, 20], [1, 16]], 0, 0)
    iota("ia", T.ia[:], [[1, 128]], 0, 0)
    iota("ioj", T.ioj[:], [[1, 320]], -160, 0)
    iota("c8", T.c8[:], [[0, 3], [1, 8]], 0, 0)
    iota("cj", T.cj[:, 0:3], [[-128, 3]], 0, -1)
    iota("dig", T.dig[:], [[0, 80]], 0, 0)
    iota("sp", T.sp[:], [[0, 24]], 0, 0)
    iota("kr", T.kr[:], [[0, 1280]], 0, 0)
    iota("negj", T.negj[:], [[-1, 320]], 0, 0)
    iota("cc", T.cc[:], [[0, 1280]], 0, 0)
    iota("iok", T.iok[:], [[1, 160]], 80, 0)

    def fill(view, name, v):
        op("V", lambda e: e.memset(view, v), [], [name])
    fill(T.ct[:], "ct", 0.0)
    ts(T.pi[:, 1:2], T.pi[:, 0:1], 15, A.bitwise_and, [("pi", 0, 1)], [("pi", 1, 2)])
    ts(T.pi[:, 2:3], T.pi[:, 0:1], 4, A.logical_shift_right, [("pi", 0, 1)], [("pi", 2, 3)])
    ts(T.pi[:, 5:6], T.pi[:, 0:1], 31, A.bitwise_and, [("pi", 0, 1)], [("pi", 5, 6)])
    ts(T.pi[:, 4:5], T.pi[:, 2:3], 1, A.bitwise_and, [("pi", 2, 3)], [("pi", 4, 5)])
    copy("V", T.pf[:, 0:3], T.pi[:, 0:3], [("pi", 0, 3)], [("pf", 0, 3)])
    copy("V", T.pf[:, 4:6], T.pi[:, 4:6], [("pi", 4, 6)], [("pf", 4, 6)])
    ts(T.pf[:, 3:4], T.pf[:, 4:5], 0.0, A.is_equal, [("pf", 4, 6)], [("pf", 3, 4)])
    pcol, kcol, gcol, even, odd, scol = (T.pf[:, i:i + 1] for i in range(6))
    copy("V", T.uoff[:], T.ui[:], ["ui"], ["uoff"])
    quant("qu", "su", "uin", 128)
    for i in (2, 1, 0):
        a, z, off = 128 * i, 128 * i + 128, T.uoff[:, 8 * i:8 * i + 8]
        op("V", lambda e: e.tensor_copy(T.qu3[:, a:z].bitcast(dt.uint32), T.qu[:, 0:128].bitcast(dt.uint32).indirect(off)), ["qu", "uoff"], [("qu3", a, z)])
        op("S", lambda e: e.activation(T.su3[:, a:z], T.su[:, 0:128].indirect(off), F.Copy), ["su", "uoff"], [("su3", a, z)])
        if i == 2:
            quant("qx", "sx", "x0", C)
    ts(T.big[:], T.k16[:], scol, A.is_gt, ["k16", "pf"], ["big"], odd, A.max)
    ts(T.big[:], T.big[:], -2 * BIG, A.mult, ["big"], ["big"], BIG, A.add)

    def late_constants():
        ts(T.ident[:], T.ia[:], pcol, A.is_equal, ["ia", "pf"], ["ident"])
        for b in range(4):
            copy("V", T.ct[:, 512 * b + b:512 * b + 512:4], T.ident[:], ["ident"], [("ct", 512 * b, 512 * b + 512)])
        fill(T.ct[:, 2560:3072:4], ("ct", 2560, 2561), 8192.0)
        fill(T.ct[:, 2561:3072:4], ("ct", 2561, 2562), 512.0)
        fill(T.ct[:, 3072:3584], ("ct", 3072, 3584), 1.0)
        ts(T.ct[:, 2048:2560:4], T.k16[:, 0:128], kcol, A.is_equal, ["k16", "pf"], [("ct", 2048, 2049)], 16.0, A.mult)
        ts(T.ct[:, 2049:2560:4], T.k16[:, 0:128], kcol, A.is_equal, ["k16", "pf"], [("ct", 2049, 2050)])
        quant("qc", "sc", "ct", 512)
        quant("qc", "sc", "ct", 384, 512)
        ts(T.bigb[:], T.k16[:, 0:160], kcol, A.is_ge, ["k16", "pf"], ["bigb"], 2000.0, A.mult)
        ts(T.bigb[:], T.bigb[:], -1000.0, A.add, ["bigb"], ["bigb"])
        ts(T.gm[:], T.ia[:, 0:8], gcol, A.is_equal, ["ia", "pf"], ["gm"])
        ts(T.maskc[:], T.c8[:], gcol, A.is_equal, ["c8", "pf"], ["maskc"])
        quant("qv", "sv", "vin", 128)

    QC, QX = ("qc", "sc"), ("qx", "sx")

    def wrapped(qs, row, rname, n, buf, bt):
        if qs:
            copy(qs[0], T[buf][:, 0:n, 0:16], row, [rname, "pf"], [(buf, 0, 1)], even)
            copy(qs[1], T[buf][:, 0:n, 16:32], row, [rname, "pf"], [(buf, 1, 2)], odd)
        if bt:
            op("V", lambda e: e.transpose(T[bt][:], T[buf][:]), [buf], [bt])

    for t in range(R):
        xc, xn = "x%d" % t, "x%d" % (t + 1)
        X = T[xc]
        if t:
            quant("qx", "sx", xc, C)
        iota("mw", T.mw[:, 0:C], [[1, C]], -240, 0)
        for bank, s0 in (("psB", 256), ("psA", 128), ("psS", 0), ("psV", 0)):
            op("T", lambda e: e.matmul_mx(T[bank][:, 0:C], T.qu3[:, s0:s0 + 128], T.su3[:, s0:s0 + 128], T.qx[:, 0:C], T.sx[:, 0:C], True, True),
               [("qu3", s0, s0 + 128), ("su3", s0, s0 + 128), "qx", "sx"], [bank])
        tt(T.r32[:, :, 16:32], T.psB[:, 0:C], T.big[:], A.max, ["psB", "big"], [("r32", 1, 2)])
        tt(T.r32[:, :, 0:16], T.psA[:, 0:C], T.big[:], A.max, ["psA", "big"], [("r32", 0, 1)])
        op("V", lambda e: e.transpose(T.rt[:], T.r32[:]), ["r32"], ["rt"])
        op("S", lambda e: e.activation(T.tt[:], T.psS[:, 0:C], F.Abs, bias=2.0 ** -120, scale=1.25 * 2.0 ** -24), ["psS"], ["tt"])
        copy("S", T.w[:, 0:C], T.psS[:, 0:C], ["psS"], [("w", 0, C)])
        ts(T.neg[:], T.rt[:, :, 16], -1.0, A.mult, ["rt"], ["neg"])
        tt(T.w[:, C:2 * C], T.psV[:, 0:C], T.tt[:], A.add, ["psV", "tt"], [("w", C, 2 * C)])
        tt(T.cmp[:, :, 0:16], T.rt[:, :, 0:16], T.psV[:, 0:C], A.is_equal, ["rt", "psV"], [("cmp", 336 * c, 336 * c + 16) for c in range(20)])
        for c in range(NS):
            lo, hi = 336 * c, 336 * c + 336
            op("S", lambda e: e.activation(T.cmp[:, c, 16:336], T.w[:, 16 * c:16 * c + C], F.Sign, bias=T.neg[:, c:c + 1]), ["w", "neg"], [("cmp", lo + 16, hi)])
            if c:
                op("S", lambda e: e.activation(T.junk[:, c % 4, :], T.cmp[:, c - 1, :], F.Relu, accum_out=T.q[:, c - 1:c]), [("cmp", lo - 336, lo)], [("junk", c % 4, c % 4 + 1), ("q", c - 1, c)])
        op("S", lambda e: e.activation(T.junk[:, 0, :], T.cmp[:, NS - 1, :], F.Relu, accum_out=T.q[:, NS - 1:NS]), [("cmp", 336 * NS - 336, 336 * NS)], [("junk", 0, 1), ("q", NS - 1, NS)])

        def total(c):
            op("V", lambda e: e.tensor_tensor_scan(T.scan[:, c, :], T.cmp[:, c, 0:168], T.cmp[:, c, 168:336], -160.0, A.add, A.add), [("cmp", 336 * c, 336 * c + 336)], [("scan", c, c + 1)])
        for c in range(NS, 20):
            ts(T.cmp[:, c, 16:336], T.w[:, 16 * c:16 * c + C], T.rt[:, c, 16:17], A.is_gt, ["w", "rt"], [("cmp", 336 * c + 16, 336 * c + 336)])
            if c > NS:
                total(c - 1)
        total(19)
        if t == 0:
            late_constants()
        ts(T.q[:, NS:20], T.scan[:, NS:20, 167], 160.0, A.add, ["scan"], [("q", NS, 20)])
        for b in range(4):
            mm(T.psD[:, 512 * b:512 * b + C], ("psD", 512 * b, 512 * b + 512), QC, 128 * b, QX, C)
        ts(T.y0[:], T.q[:], 0.0625, A.mult, ["q"], ["y0"], MAGIC, A.add)
        copy("V", T.qoff[:], T.q[:], ["q"], ["qoff"])
        ts(T.m0[:], T.y0[:], -MAGIC, A.add, ["y0"], ["m0"], -16.0, A.mult)
        ts(T.dig[:, 0:80:4], T.y0[:], -(MAGIC + 10), A.add, ["y0"], [("dig", 0, 1)])
        tt(T.dig[:, 1:80:4], T.q[:], T.m0[:], A.add, ["q", "m0"], [("dig", 1, 2)])
        for h in range(8):
            copy("S" if h in (1, 3, 5) else "V", T.mq[:, 80 * h:80 * h + 80], T.dig[:], ["dig", "gm"], [("mq", h, h + 1)], T.gm[:, h:h + 1])
        ts(T.qp[:], T.q[:], -160.0, A.add, ["q"], ["qp"])
        quant("qm", "sm", "mq", M)
        mm(T.psA[:, 0:M], "psA", QC, 512, ("qm", "sm"), M)
        op("V", lambda e: e.tensor_copy(T.orow[:, 0:C].indirect(T.qoff[:, 0:20]), T.ioj[:]), ["qoff", "ioj"], ["orow"])
        for b in range(4):
            copy("S", T.tp[:, C * b:C * b + C], T.psD[:, 512 * b:512 * b + C], [("psD", 512 * b, 512 * b + 512)], [("tp", C * b, C * b + C)])
        copy("V", T.qa[:], T.psA[:, 80:160], ["psA"], ["qa"])
        tt(T.b1[:, 0, :], T.psA[:, 0:80], T.qa[:], A.min, ["psA", "qa"], [("b1", 0, 1)])
        tt(T.b1[:, 1, :], T.psA[:, 0:80], T.qa[:], A.max, ["psA", "qa"], [("b1", 1, 2)])
        tt(T.ss[:, 0:4:3, :], T.b1[:, :, 0:40], T.b1[:, :, 40:80], A.max, ["b1"], [("ss", 0, 1), ("ss", 3, 4)])
        tt(T.ss[:, 1:6:4, :], T.b1[:, :, 0:40], T.b1[:, :, 40:80], A.min, ["b1"], [("ss", 1, 2), ("ss", 5, 6)])
        s = lambda i: ("ss", i, i + 1)
        tt(T.hi[:], T.ss[:, 3, 0:20], T.ss[:, 3, 20:40], A.max, [s(3)], ["hi"])
        tt(T.lo[:], T.ss[:, 1, 0:20], T.ss[:, 1, 20:40], A.min, [s(1)], ["lo"])
        tt(T.ss[:, 2, :], T.ss[:, 0, :], T.ss[:, 5, :], A.min, [s(0), s(5)], [s(2)])
        tt(T.sp[:, 0:20], T.hi[:], T.lo[:], A.subtract, ["hi", "lo"], ["sp"])
        tt(T.ss[:, 4, :], T.ss[:, 0, :], T.ss[:, 5, :], A.max, [s(0), s(5)], [s(4)])
        tt(T.spm[:], T.sp[:], T.maskc[:], A.mult, ["sp", "maskc"], ["spm"])
        tt(T.mn[:, 0, :], T.ss[:, 1:3, 0:20], T.ss[:, 3:5, 20:40], A.min, ["ss"], [("mn", 0, 1)])
        tt(T.s4[:], T.spm[:, :, 0:4], T.spm[:, :, 4:8], A.add, ["spm"], ["s4"])
        tt(T.mn[:, 1, :], T.ss[:, 3:5, 0:20], T.ss[:, 1:3, 20:40], A.min, ["ss"], [("mn", 1, 2)])
        tt(T.s2[:], T.s4[:, :, 0:2], T.s4[:, :, 2:4], A.add, ["s4"], ["s2"])
        tt(T.mx[:, 0, :], T.ss[:, 1:3, 0:20], T.ss[:, 3:5, 20:40], A.max, ["ss"], [("mx", 0, 1)])
        tt(T.v3[:, 0:3], T.s2[:, :, 0], T.s2[:, :, 1], A.add, ["s2"], ["v3"])
        tt(T.mx[:, 1, :], T.ss[:, 3:5, 0:20], T.ss[:, 1:3, 20:40], A.max, ["ss"], [("mx", 1, 2)])
        ts(T.y3[:, 0:3], T.v3[:, 0:3], 0.0625, A.mult, ["v3"], ["y3"], MAGIC, A.add)
        tt(T.mn2[:], T.mn[:, 0, :], T.mn[:, 1, :], A.max, ["mn"], ["mn2"])
        ts(T.l3[:, 0:3], T.y3[:, 0:3], -MAGIC, A.add, ["y3"], ["l3"], -16.0, A.mult)
        ts(T.h3[:, 0:3], T.y3[:, 0:3], -(MAGIC + 10), A.add, ["y3"], ["h3"])
        tt(T.l3[:, 0:3], T.l3[:, 0:3], T.v3[:, 0:3], A.add, ["l3", "v3"], ["l3"])
        for d in range(6):
            e3 = d % 3
            n = min(128, C - 128 * e3)
            a, z = 512 * e3 + d // 3, 512 * e3 + 4 * n
            src = "l3" if d > 2 else "h3"
            copy("V", T.kr[:, a:z:4], T.ident[:, 0:n], ["ident", src], [("kr", d, d + 1)], T[src][:, e3:e3 + 1])
        quant("qk", "sk", "kr", C)
        mm(T.psB[:, 0:C], "psB", QC, 640, ("qk", "sk"), C)
        ts(T.ok[:, 0:3], T.v3[:, 0:3], -160.0, A.add, ["v3"], ["ok"], 512.0, A.mult)
        tt(T.mx2[:], T.mx[:, 0, :], T.mx[:, 1, :], A.min, ["mx"], ["mx2"])
        tt(T.ma[:], T.mn2[:, 0:20], T.mn2[:, 20:40], A.max, ["mn2"], ["ma"])
        tt(T.mb[:], T.mx2[:, 0:20], T.mx2[:, 20:40], A.min, ["mx2"], ["mb"])
        tt(T.ok[:, 0:3], T.ok[:, 0:3], T.cj[:, 0:3], A.add, ["ok", "cj"], ["ok"])
        tt(T.z0[:], T.ma[:], T.mb[:], A.add, ["ma", "mb"], ["z0"])
        tt(T.z0[:], T.z0[:], T.qp[:], A.subtract, ["z0", "qp"], ["z0"])
        tt(T.z0[:], T.z0[:], T.mb[:], A.min, ["z0", "mb"], ["z0"])
        tt(T.z0[:], T.z0[:], T.ma[:], A.max, ["z0", "ma"], ["z0"])
        ts(T.woff[:], T.z0[:], 160.0, A.add, ["z0"], ["woff"])
        tt(T.key[:], T.psB[:, 0:C], T.negj[:], A.add, ["psB", "negj"], ["key"])
        for e3 in range(3):
            ts(T.cc[:, e3:1280:4], T.key[:], T.ok[:, e3:e3 + 1], A.is_lt, ["key", "ok"], [("cc", e3, e3 + 1)])
        quant("qn", "sn", "cc", C)
        mm(T.psS[:, 0:C], "psS", QC, 768, ("qn", "sn"), C)
        op("V", lambda e: e.tensor_copy(T.lrow[:], T.orow[:, 0:C].indirect(T.woff[:, 0:20])), ["woff", "orow"], ["lrow"])
        ts(T.rb[:, :, 0:16], T.psS[:, 0:C], -160.0, A.add, ["psS"], [("rb", 0, 1)])
        copy("V", T.rb[:, :, 16:32], T.rb[:, :, 0:16], [("rb", 0, 1)], [("rb", 1, 2)])
        wrapped("SS", T.lrow[:], "lrow", 20, "yb", None)
        op("V", lambda e: e.transpose(T.rbt[:], T.rb[:]), ["rb"], ["rbt"])
        ts(T.roff[:], T.rbt[:, :, 0], 160.0, A.add, ["rbt"], ["roff"])
        op("V", lambda e: e.tensor_copy(T.lcrow[:, 0:C].indirect(T.roff[:, 0:20]), T.lrow[:]), ["roff", "lrow"], ["lcrow"])
        wrapped("VV", T.lcrow[:, 0:M], "lcrow", 10, "lb", "lbt")
        tt(T.lcw[:], T.lbt[:, :, 0], T.lbt[:, :, 16], A.add, ["lbt"], ["lcw"])
        ts(T.lcoff[:], T.lcw[:], 160.0, A.add, ["lcw"], ["lcoff"])
        for b in range(4):
            copy("V" if b % 2 else "S", T.z[:, b:640:4], T.tp[:, C * b:C * b + C].indirect(T.lcoff[:, 0:10]), ["lcoff", ("tp", C * b, C * b + C)], [("z", b, b + 1)])
        tt(T.dl[:], T.lcrow[:, 0:M], T.bigb[:], A.max, ["lcrow", "bigb"], ["dl"])
        qz, sz, lq, lp = "qz%d" % t, "sz%d" % t, "lq%d" % t, "ls%d" % t
        quant(qz, sz, "z", M)
        dst = T.cores[(rank + 1 + t) % N]
        rid, pid = topo.addr(dst, core)
        mask, ne = topo.mask(core, dst), len(topo.engines(core, dst))
        sent, came = "sent%d" % t, "came%d" % t
        waits("G", "net", [qz, sz], [])
        g.remote_dma(T[lq][:, 0:M].bitcast(dt.uint8), T[qz][:, 0:M].bitcast(dt.uint8), T.sem[came], T.sem[sent], pid, rid, mask)
        g.remote_dma(T[lp][:, 0:M], T[sz][:, 0:M], T.sem[came], T.sem[sent], pid, rid, mask)
        count[sent] = 2 * ne
        back = T.cores[(rank - 1 - t) % N]
        count[came] = 2 * len(topo.engines(back, core))
        note(None, "net", came, count[came], [], [lq, lp])
        tt(T.lcb[:], T.lbt[:, :, 0:16], T.lbt[:, :, 16:32], A.add, ["lbt"], ["lcb"])
        tt(T.cd[:, :, 0:16], T.lcb[:], T.dl[:], A.is_equal, ["lcb", "dl"], [("cd", 176 * c, 176 * c + 16) for c in range(10)])
        for c in range(10):
            n = 16 + 16 * c
            if c:
                ts(T.cd[:, c, 16:n], T.lcrow[:, 0:16 * c], T.lcw[:, c:c + 1], A.is_equal, ["lcrow", "lcw"], [("cd", 176 * c + 16, 176 * c + 176)])
            op("S", lambda e: e.activation(T.junk[:, c % 4, 0:n], T.cd[:, c, 0:n], F.Copy, scale=320.0, accum_out=T.dup[:, c:c + 1]), [("cd", 176 * c, 176 * c + 176)], [("junk", c % 4, c % 4 + 1), ("dup", c, c + 1)])
        wrapped("", None, "lrow", 20, "yb", "ybt")
        tt(T.lw[:], T.ybt[:, :, 0], T.ybt[:, :, 16], A.add, ["ybt"], ["lw"])
        ts(T.loff[:], T.lw[:], 160.0, A.add, ["lw"], ["loff"])
        for b in range(4):
            op("V", lambda e: e.tensor_tensor(T.yt[:, C * b:C * b + C], T.tp[:, C * b:C * b + C].indirect(T.loff[:, 0:20]), X[:, b:1280:4], A.add), ["loff", ("tp", C * b, C * b + C), xc], [("yt", b, b + 1)])
            copy("S", T.yh[:, 480 * b:480 * b + C], T.yt[:, C * b:C * b + C], [("yt", b, b + 1)], [("yh", 480 * b, 480 * b + C)], 0.5)
        tt(T.dof[:], T.dup[:], T.lcw[:], A.add, ["dup", "lcw"], ["dof"])
        ts(T.doff[:], T.dof[:], 160.0, A.add, ["dof"], ["doff"])
        op("V", lambda e: e.tensor_copy(T.mw[:, 0:2880].indirect(T.doff[:, 0:10]), T.iok[:]), ["doff", "iok"], ["mw"])
        wrapped("VV", T.mw[:, 0:C], "mw", 20, "xb", "xbt")
        tt(T.mwf[:], T.xbt[:, :, 0], T.xbt[:, :, 16], A.add, ["xbt"], ["mwf"])
        ts(T.moff[:], T.mwf[:], 240.0, A.add, ["mwf"], ["moff"])
        if t == R - 1:
            op("S", lambda e: e.activation(T.tt[:], T.lrow[:], F.Identity, bias=160.0), ["lrow"], ["tt"])
            dma("Y", T.ol[:], T.tt[0:128:16, :], ["tt"], [])
        for b in range(4):
            bank = ("psD", 512 * b, 512 * b + 512)
            mm(T.psD[:, 512 * b:512 * b + M], bank, ("wq", "wp"), 128 * b, (lq, lp), M)
        for b in range(4):
            bank = ("psD", 512 * b, 512 * b + 512)
            copy("V" if b % 2 else "S", T.yh[:, 480 * b + C:480 * b + 480], T.psD[:, 512 * b:512 * b + M], [bank], [("yh", 480 * b + C, 480 * b + 480)], 0.03125)
        for b in range(4):
            copy("V" if b % 2 else "S", T[xn][:, b:1280:4], T.yh[:, 480 * b:480 * b + 480].indirect(T.moff[:, 0:20]), ["moff", ("yh", 480 * b, 480 * b + 480)], [(xn, b, b + 1)])

    quant("qx", "sx", "x%d" % R, C)
    mm(T.psA[:, 0:C], "psA", ("qv", "sv"), 0, QX, C)
    dma("Y", T.oc[:], T.qx[:].bitcast(dt.uint8), ["qx"], [])
    copy("V", T.key[:], T.psA[:, 0:C], ["psA"], ["key"])
    for k in range(4):
        dma("S" if k % 2 else "Y", T.osc[4 * k:4 * k + 4, :], T.sx[32 * k:32 * k + 4, :], ["sx"], [])
    dma("S", T.y[:], T.key[:], ["key"], [])
    finish()
